import numpy as np
import ml_dtypes


def mxq(x, axis, fmt="e4m3"):
    dtype, down = {"e4m3": (ml_dtypes.float8_e4m3fn, 7), "e5m2": (ml_dtypes.float8_e5m2, 14)}[fmt]
    v = np.moveaxis(np.asarray(x, np.float32).astype(ml_dtypes.bfloat16).astype(np.float64), axis, -1)
    blocks = v.reshape(v.shape[:-1] + (-1, 32))
    amax = np.abs(blocks).max(-1, keepdims=True)
    byte = np.maximum(np.where(amax > 0, np.frexp(amax)[1] - 1 + 127, 0) - down, 1)
    scale = np.exp2(byte - 127.0)
    codes = (blocks / scale).astype(np.float32).astype(dtype).astype(np.float64)
    return np.moveaxis((codes * scale).reshape(v.shape), -1, axis)


WIDE = False


def mx_kscale(k):
    if not WIDE:
        return np.ones(k)
    levels = np.array([10, -10, 5, -5, 0])
    if k % 512:
        return np.exp2(np.random.permutation(np.resize(levels, k // 32))).repeat(32)
    a = np.empty((k // 512, 16))
    for p in range(k // 512):
        a[p, :8] = np.random.permutation(np.resize(levels, 8))
        for g in range(8):
            far = levels[np.abs(levels - a[p, g]) >= 10]
            a[p, g + 8] = far[np.random.randint(len(far))]
    return np.exp2(a.ravel()).repeat(32)


def f64(x):
    return np.asarray(x).astype(np.float64)


def striped(idx):
    return np.tile(idx.reshape(-1, 16).T, (8, 1)).astype(np.uint16)


def unstriped(offs):
    return offs[:16].T.reshape(-1).astype(np.int64)


def striped8(idx):
    return np.concatenate([x.reshape(-1, 16).T for x in idx]).astype(np.uint16)


def runs(offs, k):
    lists = np.stack([offs[16 * r : 16 * r + 16].T.reshape(-1) for r in range(8)]).astype(np.int64)
    return lists[np.arange(k) % 512 // 64]


def pack_weight(w):
    k, n = w.shape
    w = f64(np.asarray(w, np.float32).astype(ml_dtypes.bfloat16)).reshape(k // 32, 32, n)
    amax = np.abs(w).max(1)
    byte = np.clip(np.where(amax > 0, np.frexp(amax)[1] - 1 + 127 - 7, 1), 1, 254)
    scaled = (w * np.exp2(127.0 - byte)[:, None, :]).reshape(k, n).astype(np.float32)
    words = np.ascontiguousarray(scaled.reshape(k // 512, 128, 4, n).transpose(0, 1, 3, 2)).astype(ml_dtypes.float8_e4m3fn).view(np.uint8)
    return words, np.ascontiguousarray(byte.astype(np.uint8).reshape(k // 512, 16, n))


def unpack_weight(words, scales):
    g, p, n, _ = words.shape
    vals = np.ascontiguousarray(words).view(ml_dtypes.float8_e4m3fn).astype(np.float64) * np.repeat(np.exp2(scales.astype(np.float64) - 127.0), 8, axis=1)[..., None]
    return vals.transpose(0, 1, 3, 2).reshape(g * 512, n)


def sigmoid(v):
    return 1.0 / (1.0 + np.exp(-np.maximum(v, -700.0)))

def planes(y):
    n, m = y.shape
    v = y.astype(np.float32).astype(ml_dtypes.bfloat16).astype(np.float64).reshape(n // 32, 32, m)
    top = np.abs(v).max(1)
    byte = np.clip(np.where(top > 0, np.frexp(top)[1] - 1 + 127 - 7, 1), 1, 254)
    codes = (v * np.exp2(127.0 - byte)[:, None, :]).reshape(n, m).astype(np.float32).astype(ml_dtypes.float8_e4m3fn).view(np.uint8)
    words = codes.reshape(n // 512, 128, 4, m).transpose(0, 1, 3, 2)
    return np.ascontiguousarray(words), np.ascontiguousarray(byte.astype(np.uint8).reshape(n // 512, 16, m))


K, T, S, N, H, W = 512, 2048, 512, 512, 512, 256


def setup_inputs():
    n = np.random.standard_normal
    s = mx_kscale(K)[:, None]
    u = mx_kscale(H)
    packed_xT = pack_weight(n((K, T)) * s)
    packed_w1 = pack_weight(n((K, H)) / np.sqrt(K) / s)
    packed_w2 = pack_weight(n((H, N)) / np.sqrt(H) / u[:, None])
    packed_w3 = pack_weight(n((H, N)) / np.sqrt(H) / u[:, None])
    perm = np.stack([np.random.permutation(S) for _ in range(8)])
    return {
        "x_words": packed_xT[0],
        "x_scales": packed_xT[1],
        "w1_words": packed_w1[0],
        "w1_scales": packed_w1[1],
        "gn": (np.random.uniform(0.5, 1.5, (H, 1)) * u[:, None]).astype(np.float32),
        "w2_words": packed_w2[0],
        "w2_scales": packed_w2[1],
        "gm": (np.random.uniform(0.5, 1.5, (H, 1)) * u[:, None]).astype(np.float32),
        "w3_words": packed_w3[0],
        "w3_scales": packed_w3[1],
        "offs": striped(np.random.permutation(T)[:S]),
        "n1": striped8(perm[:, :W]),
        "n2": striped8(perm[:, W:]),
        "n3": striped8(np.stack([np.random.permutation(S) for _ in range(8)])),
        "n4": striped8(np.stack([np.random.permutation(S) for _ in range(8)])),
        "n5": striped8(np.stack([np.random.permutation(S) for _ in range(8)])),
        "n6": striped8(np.stack([np.random.permutation(S) for _ in range(8)])),
        "n7": striped8(np.stack([np.random.permutation(S) for _ in range(8)])),
    }


def reference(x_words, x_scales, w1_words, w1_scales, gn, w2_words, w2_scales, gm, w3_words, w3_scales, offs, n1, n2, n3, n4, n5, n6, n7):
    xq = unpack_weight(x_words, x_scales)[:, unstriped(offs)]
    y = unpack_weight(w1_words, w1_scales).T @ xq
    pa = y[np.arange(H)[:, None], runs(n1, H)]
    pb = y[np.arange(H)[:, None], runs(n2, H)]
    ra = pa * sigmoid(pb)
    ds = y.copy()
    ds[np.arange(H)[:, None], runs(n2, H)] = ra
    z = f64(gn) * ds
    a = unpack_weight(w2_words, w2_scales).T @ mxq(z, 0, "e4m3")
    ex = np.exp(0.5 * y)
    z2 = f64(gm) * (np.log((ex + ex[np.arange(H)[:, None], runs(n3, H)]) / (ex[np.arange(H)[:, None], runs(n4, H)] + ex[np.arange(H)[:, None], runs(n5, H)])))
    b = unpack_weight(w3_words, w3_scales).T @ mxq(z2, 0, "e4m3")
    out_0 = (a - (a[np.arange(N)[:, None], runs(n6, N)])) / (np.abs(b) + np.abs(b[np.arange(N)[:, None], runs(n7, N)]) + 0.5)
    return (out_0,) + planes(out_0)

@@ -1,0 +1,223 @@
+from contextlib import ExitStack
+
+import concourse.mybir as mybir
+
+F32 = mybir.dt.float32
+BF16 = mybir.dt.bfloat16
+I32 = mybir.dt.int32
+U32 = mybir.dt.uint32
+U16 = mybir.dt.uint16
+U8 = mybir.dt.uint8
+FP8X4 = mybir.dt.float8_e4m3fn_x4
+ACT = mybir.ActivationFunctionType
+ALU = mybir.AluOpType
+
+P = 128
+PACK = 4
+T = 2048
+S = 512
+HALF = S // 2
+LIST_HALF = HALF // 16
+SCALAR_N3 = 1
+
+FLOPS = 3 * 2 * 512 * 512 * 512
+
+
+def tile_picked_forknormbfoldodds_none_po_kernel(
+    tc, x_words, x_scales, w1_words, w1_scales, gn, w2_words, w2_scales, gm, w3_words, w3_scales,
+    offs, n1, n2, n3, n4, n5, n6, n7, out_0, out_1, out_2,
+):
+    nc = tc.nc
+    with ExitStack() as ctx:
+        sb = ctx.enter_context(tc.tile_pool(name="sb", bufs=1))
+        ps = ctx.enter_context(tc.psum_pool(name="ps", bufs=1))
+
+        def planes(name, width=S):
+            return [sb.tile([P, width], F32, name=f"{name}{t}", align_bytes=64) for t in range(PACK)]
+
+        def load_list(name, src):
+            tile = sb.tile(list(src.shape), U16, name=name)
+            nc.sync.dma_start(tile[:], src)
+            return tile
+
+        def load_words(name, src):
+            tile = sb.tile([P, src.shape[2]], I32, name=name, align_bytes=64)
+            nc.sync.dma_start(tile[:], src[0].rearrange("p n r -> p (n r)").bitcast(I32))
+            return tile
+
+        def load_scale_rows(queues, tile, first, src):
+            for q in range(4):
+                queues[q].dma_start(
+                    tile[32 * q + first : 32 * q + first + 4, :].bitcast(I32),
+                    src[0, 4 * q : 4 * q + 4, :].bitcast(I32),
+                )
+
+        def load_gain(name, src):
+            tile = sb.tile([P, PACK], F32, name=name)
+            nc.sync.dma_start(tile[:], src.rearrange("(p t) o -> p (t o)", t=PACK))
+            return tile
+
+        def deal(name, src, dtype):
+            tile = sb.tile([P, S], dtype, name=name, align_bytes=64)
+            nc.vector.tensor_copy(
+                tile[:].rearrange("p (t m) -> p t m", t=PACK),
+                src[:].rearrange("p (m t) -> p t m", t=PACK),
+            )
+            return tile
+
+        def half(offsets, h):
+            return offsets[:, h * LIST_HALF : (h + 1) * LIST_HALF]
+
+        def cols(h):
+            return slice(h * HALF, (h + 1) * HALF)
+
+        def product(tag, w, w_scale, first, codes, scale):
+            banks = []
+            for t in range(PACK):
+                bank = ps.tile([P, S], F32, name=f"{tag}{t}", tag=f"{tag}{t}")
+                m = slice(t * P, (t + 1) * P)
+                nc.tensor.matmul_mx(
+                    out=bank[:], lhsT=w[:, m].bitcast(FP8X4), lhsT_scale=w_scale[first:P, m],
+                    rhs=codes[:].bitcast(FP8X4), rhs_scale=scale[:], start=True, stop=True,
+                )
+                banks.append(bank)
+            return banks
+
+        def quantise(name, src, codes, scale):
+            width = src.shape[2]
+            woven = sb.tile([P, width, PACK], BF16, name=name, align_bytes=64)
+            nc.vector.tensor_copy(woven[:], src.rearrange("p t c -> p c t"))
+            nc.vector.quantize_mx(
+                out=codes.bitcast(FP8X4), scales=scale, in_=woven[:].rearrange("p c t -> p (c t)")
+            )
+
+        xs_raw = sb.tile([P, T], U8, name="xs_raw", align_bytes=64)
+        w1s_raw = sb.tile([P, S], U8, name="w1s_raw", align_bytes=64)
+        w23s_raw = sb.tile([P, S], U8, name="w23s_raw", align_bytes=64)
+        nc.vector.memset(w1s_raw[:].bitcast(I32), 0)
+        nc.vector.memset(xs_raw[:].bitcast(I32), 0)
+        warm = sb.tile([P, 1], F32, name="warm")
+        nc.vector.memset(warm[:], 1.0)
+        nc.scalar.activation(warm[:], warm[:], ACT.Exp)
+        on_sync = [nc.sync] * 4
+        load_scale_rows(on_sync, xs_raw, 0, x_scales)
+        load_scale_rows([nc.sync, nc.sync, nc.gpsimd, nc.gpsimd], w1s_raw, 0, w1_scales)
+        offs_t = load_list("offs_t", offs)
+        w1_raw = load_words("w1_raw", w1_words)
+        xw_raw = load_words("xw_raw", x_words)
+        n4_t = load_list("n4_t", n4)
+        n5_t = load_list("n5_t", n5)
+        n1_t = load_list("n1_t", n1)
+        n3_t = load_list("n3_t", n3)
+        n2_t = load_list("n2_t", n2)
+        w3_raw = load_words("w3_raw", w3_words)
+        w2_raw = load_words("w2_raw", w2_words)
+        nc.vector.memset(w23s_raw[:].bitcast(I32), 0)
+        load_scale_rows(on_sync, w23s_raw, 0, w2_scales)
+        load_scale_rows(on_sync, w23s_raw, 4, w3_scales)
+        gm_t = load_gain("gm_t", gm)
+        gn_t = load_gain("gn_t", gn)
+        n6_t = load_list("n6_t", n6)
+        n7_t = load_list("n7_t", n7)
+
+        w1_scale = deal("w1_scale", w1s_raw, U8)
+        w1 = deal("w1", w1_raw, I32)
+        x_scale = sb.tile([P, S], U8, name="x_scale", align_bytes=64)
+        x_codes = sb.tile([P, S], U32, name="x_codes", align_bytes=64)
+        nc.vector.tensor_copy(x_scale[:], xs_raw[:].indirect(offs_t[:]))
+        nc.vector.tensor_copy(x_codes[:], xw_raw[:].bitcast(U32).indirect(offs_t[:]))
+        y_ps = product("lo", w1, w1_scale, 0, x_codes, x_scale)
+
+        y = planes("y")
+        ds = planes("ds")
+        ex = planes("ex")
+        e3 = planes("e3")
+        e4 = planes("e4")
+        odds = planes("odds", 2 * S)
+        pa = planes("pa", HALF)
+        for t in range(PACK):
+            nc.scalar.copy(y[t][:], y_ps[t][:])
+            nc.scalar.activation(ex[t][:], y_ps[t][:], ACT.Exp, scale=0.5)
+            if t < PACK - SCALAR_N3:
+                nc.sync.dma_start(e3[t][:], ex[t][:])
+            for h in range(2):
+                nc.scalar.activation(e4[t][:, cols(h)], y[t][:].indirect(half(n4_t, h)), ACT.Exp, scale=0.5)
+            nc.sync.dma_start(ds[t][:], y[t][:])
+        for t in range(PACK - SCALAR_N3, PACK):
+            for h in range(2):
+                nc.scalar.activation(e3[t][:, cols(h)], y[t][:].indirect(half(n3_t, h)), ACT.Exp, scale=0.5)
+        for t in range(PACK):
+            for h in range(2):
+                nc.vector.tensor_tensor(
+                    odds[t][:, S + h * HALF : S + (h + 1) * HALF], ex[t][:].indirect(half(n5_t, h)), e4[t][:, cols(h)], ALU.add
+                )
+            if t < PACK - SCALAR_N3:
+                for h in range(2):
+                    nc.vector.tensor_tensor(odds[t][:, cols(h)], ex[t][:].indirect(half(n3_t, h)), e3[t][:, cols(h)], ALU.add)
+            else:
+                nc.vector.tensor_tensor(odds[t][:, 0:S], ex[t][:], e3[t][:], ALU.add)
+
+        gate = planes("gate", HALF)
+        for t in range(PACK):
+            nc.vector.tensor_copy(pa[t][:], y[t][:].indirect(n1_t[:]))
+            nc.scalar.activation(gate[t][:], y[t][:].indirect(n2_t[:]), ACT.Sigmoid)
+        w23_scale = deal("w23_scale", w23s_raw, U8)
+        w3 = deal("w3", w3_raw, I32)
+        w2 = deal("w2", w2_raw, I32)
+
+        z2_all = sb.tile([P, PACK, S], BF16, name="z2_all", align_bytes=64)
+        z_all = sb.tile([P, PACK, S], BF16, name="z_all", align_bytes=64)
+        for t in range(PACK):
+            nc.scalar.activation(odds[t][:], odds[t][:], ACT.Ln)
+        for t in range(PACK):
+            nc.vector.tensor_tensor(ds[t][:].indirect(n2_t[:]), pa[t][:], gate[t][:], ALU.mult)
+            nc.vector.tensor_tensor(odds[t][:, 0:S], odds[t][:, 0:S], odds[t][:, S : 2 * S], ALU.subtract)
+            nc.scalar.activation(z2_all[:, t, :], odds[t][:, 0:S], ACT.Copy, scale=gm_t[:, t : t + 1])
+        for t in range(PACK):
+            nc.scalar.activation(z_all[:, t, :], ds[t][:], ACT.Copy, scale=gn_t[:, t : t + 1])
+        nc.scalar.activation(warm[:], odds[PACK - 1][:, S : S + 1], ACT.Abs_reciprocal_sqrt, scale=0.0, bias=1.0)
+        z2_codes = sb.tile([P, S], U32, name="z2_codes", align_bytes=64)
+        z2_scale = sb.tile([P, S], U8, name="z2_scale", align_bytes=64)
+        quantise("z2_woven", z2_all[:], z2_codes[:], z2_scale[:])
+        b_ps = product("hi", w3, w23_scale, 4, z2_codes, z2_scale)
+        z_codes = sb.tile([P, S], U32, name="z_codes", align_bytes=64)
+        z_scale = sb.tile([P, S], U8, name="z_scale", align_bytes=64)
+        quantise("z_woven", z_all[:], z_codes[:], z_scale[:])
+        a_ps = product("lo", w2, w23_scale, 0, z_codes, z_scale)
+
+        size = planes("size")
+        size2 = planes("size2")
+        for t in range(PACK):
+            nc.scalar.activation(size[t][:], b_ps[t][:], ACT.Abs)
+            nc.scalar.activation(size2[t][:], b_ps[t][:], ACT.Abs)
+        neg_a = planes("neg_a")
+        neg_a2 = planes("neg_a2")
+        for t in range(PACK):
+            nc.scalar.activation(neg_a[t][:], a_ps[t][:], ACT.Copy, scale=-1.0)
+            nc.sync.dma_start(neg_a2[t][:], neg_a[t][:])
+        den = planes("den")
+        for t in range(PACK):
+            for h in range(2):
+                nc.vector.tensor_tensor(den[t][:, cols(h)], size[t][:].indirect(half(n7_t, h)), size2[t][:, cols(h)], ALU.add)
+            nc.scalar.activation(den[t][:], den[t][:], ACT.Abs_reciprocal_sqrt, bias=0.5)
+            nc.scalar.activation(den[t][:], den[t][:], ACT.Square)
+        out_codes = sb.tile([P, S], I32, name="out_codes", align_bytes=64)
+        out_scale = sb.tile([P, S], U8, name="out_scale", align_bytes=64)
+        out_rows = out_0.rearrange("(p t) c -> p t c", t=PACK)
+        out_words = out_1[0].rearrange("p n r -> p (n r)").bitcast(I32)
+        for h in range(2):
+            diff = sb.tile([P, PACK, HALF], F32, name=f"diff{h}", align_bytes=64)
+            res = sb.tile([P, PACK, HALF], F32, name=f"res{h}", align_bytes=64)
+            for t in range(PACK):
+                nc.vector.tensor_tensor(diff[:, t, :], neg_a[t][:].indirect(half(n6_t, h)), neg_a2[t][:, cols(h)], ALU.subtract)
+            for t in range(PACK):
+                nc.vector.tensor_tensor(res[:, t, :], diff[:, t, :], den[t][:, cols(h)], ALU.mult)
+                if t % 2 == 1:
+                    nc.sync.dma_start(out_rows[:, t - 1 : t + 1, cols(h)], res[:, t - 1 : t + 1, :])
+            quantise(f"out_woven{h}", res[:], out_codes[:, cols(h)], out_scale[:, cols(h)])
+            nc.sync.dma_start(out_words[:, cols(h)], out_codes[:, cols(h)])
+        for q in range(4):
+            queue = nc.sync if q % 2 == 0 else nc.scalar
+            queue.dma_start(
+                out_2[0, 4 * q : 4 * q + 4, :].bitcast(I32), out_scale[32 * q : 32 * q + 4, :].bitcast(I32)
+            )

@@ -45,9 +45,9 @@ def tile_picked_forknormbfoldodds_none_po_kernel(
             nc.sync.dma_start(tile[:], src[0].rearrange("p n r -> p (n r)").bitcast(I32))
             return tile
 
-        def load_scale_rows(queues, tile, first, src):
+        def load_scale_rows(queue, tile, first, src):
             for q in range(4):
-                queues[q].dma_start(
+                queue.dma_start(
                     tile[32 * q + first : 32 * q + first + 4, :].bitcast(I32),
                     src[0, 4 * q : 4 * q + 4, :].bitcast(I32),
                 )
@@ -57,9 +57,9 @@ def tile_picked_forknormbfoldodds_none_po_kernel(
             nc.sync.dma_start(tile[:], src.rearrange("(p t) o -> p (t o)", t=PACK))
             return tile
 
-        def deal(name, src, dtype):
+        def deal(name, src, dtype, engine):
             tile = sb.tile([P, S], dtype, name=name, align_bytes=64)
-            nc.vector.tensor_copy(
+            engine.tensor_copy(
                 tile[:].rearrange("p (t m) -> p t m", t=PACK),
                 src[:].rearrange("p (m t) -> p t m", t=PACK),
             )
@@ -93,129 +93,180 @@ def tile_picked_forknormbfoldodds_none_po_kernel(
 
         xs_raw = sb.tile([P, T], U8, name="xs_raw", align_bytes=64)
         w1s_raw = sb.tile([P, S], U8, name="w1s_raw", align_bytes=64)
-        w23s_raw = sb.tile([P, S], U8, name="w23s_raw", align_bytes=64)
-        nc.vector.memset(w1s_raw[:].bitcast(I32), 0)
         nc.vector.memset(xs_raw[:].bitcast(I32), 0)
-        warm = sb.tile([P, 1], F32, name="warm")
-        nc.vector.memset(warm[:], 1.0)
-        nc.scalar.activation(warm[:], warm[:], ACT.Exp)
-        on_sync = [nc.sync] * 4
-        load_scale_rows(on_sync, xs_raw, 0, x_scales)
-        load_scale_rows([nc.sync, nc.sync, nc.gpsimd, nc.gpsimd], w1s_raw, 0, w1_scales)
-        offs_t = load_list("offs_t", offs)
+        nc.vector.memset(w1s_raw[:].bitcast(I32), 0)
+        load_scale_rows(nc.sync, xs_raw, 0, x_scales)
         w1_raw = load_words("w1_raw", w1_words)
+        offs_t = load_list("offs_t", offs)
         xw_raw = load_words("xw_raw", x_words)
+        load_scale_rows(nc.sync, w1s_raw, 0, w1_scales)
         n4_t = load_list("n4_t", n4)
-        n5_t = load_list("n5_t", n5)
+        w2_raw = load_words("w2_raw", w2_words)
+        w3_raw = load_words("w3_raw", w3_words)
         n1_t = load_list("n1_t", n1)
+        n5_t = load_list("n5_t", n5)
         n3_t = load_list("n3_t", n3)
         n2_t = load_list("n2_t", n2)
-        w3_raw = load_words("w3_raw", w3_words)
-        w2_raw = load_words("w2_raw", w2_words)
-        nc.vector.memset(w23s_raw[:].bitcast(I32), 0)
-        load_scale_rows(on_sync, w23s_raw, 0, w2_scales)
-        load_scale_rows(on_sync, w23s_raw, 4, w3_scales)
-        gm_t = load_gain("gm_t", gm)
-        gn_t = load_gain("gn_t", gn)
-        n6_t = load_list("n6_t", n6)
-        n7_t = load_list("n7_t", n7)
 
-        w1_scale = deal("w1_scale", w1s_raw, U8)
-        w1 = deal("w1", w1_raw, I32)
+        w1_scale = deal("w1_scale", w1s_raw, U8, nc.gpsimd)
+        w1 = deal("w1", w1_raw, I32, nc.vector)
         x_scale = sb.tile([P, S], U8, name="x_scale", align_bytes=64)
         x_codes = sb.tile([P, S], U32, name="x_codes", align_bytes=64)
         nc.vector.tensor_copy(x_scale[:], xs_raw[:].indirect(offs_t[:]))
         nc.vector.tensor_copy(x_codes[:], xw_raw[:].bitcast(U32).indirect(offs_t[:]))
         y_ps = product("lo", w1, w1_scale, 0, x_codes, x_scale)
 
-        y = planes("y")
+        y = planes("y", 2 * S)
+        ex = planes("ex", 2 * S)
+        size = planes("size", 2 * S)
+        neg_a = planes("neg_a", 2 * S)
         ds = planes("ds")
-        ex = planes("ex")
         e3 = planes("e3")
         e4 = planes("e4")
         odds = planes("odds", 2 * S)
         pa = planes("pa", HALF)
-        for t in range(PACK):
-            nc.scalar.copy(y[t][:], y_ps[t][:])
-            nc.scalar.activation(ex[t][:], y_ps[t][:], ACT.Exp, scale=0.5)
-            if t < PACK - SCALAR_N3:
-                nc.sync.dma_start(e3[t][:], ex[t][:])
-            for h in range(2):
-                nc.scalar.activation(e4[t][:, cols(h)], y[t][:].indirect(half(n4_t, h)), ACT.Exp, scale=0.5)
-            nc.sync.dma_start(ds[t][:], y[t][:])
-        for t in range(PACK - SCALAR_N3, PACK):
-            for h in range(2):
-                nc.scalar.activation(e3[t][:, cols(h)], y[t][:].indirect(half(n3_t, h)), ACT.Exp, scale=0.5)
-        for t in range(PACK):
-            for h in range(2):
-                nc.vector.tensor_tensor(
-                    odds[t][:, S + h * HALF : S + (h + 1) * HALF], ex[t][:].indirect(half(n5_t, h)), e4[t][:, cols(h)], ALU.add
-                )
-            if t < PACK - SCALAR_N3:
-                for h in range(2):
-                    nc.vector.tensor_tensor(odds[t][:, cols(h)], ex[t][:].indirect(half(n3_t, h)), e3[t][:, cols(h)], ALU.add)
-            else:
-                nc.vector.tensor_tensor(odds[t][:, 0:S], ex[t][:], e3[t][:], ALU.add)
-
         gate = planes("gate", HALF)
-        for t in range(PACK):
-            nc.vector.tensor_copy(pa[t][:], y[t][:].indirect(n1_t[:]))
-            nc.scalar.activation(gate[t][:], y[t][:].indirect(n2_t[:]), ACT.Sigmoid)
-        w23_scale = deal("w23_scale", w23s_raw, U8)
-        w3 = deal("w3", w3_raw, I32)
-        w2 = deal("w2", w2_raw, I32)
-
+        size2 = planes("size2")
+        neg_a2 = planes("neg_a2")
         z2_all = sb.tile([P, PACK, S], BF16, name="z2_all", align_bytes=64)
         z_all = sb.tile([P, PACK, S], BF16, name="z_all", align_bytes=64)
-        for t in range(PACK):
-            nc.scalar.activation(odds[t][:], odds[t][:], ACT.Ln)
-        for t in range(PACK):
-            nc.vector.tensor_tensor(ds[t][:].indirect(n2_t[:]), pa[t][:], gate[t][:], ALU.mult)
-            nc.vector.tensor_tensor(odds[t][:, 0:S], odds[t][:, 0:S], odds[t][:, S : 2 * S], ALU.subtract)
-            nc.scalar.activation(z2_all[:, t, :], odds[t][:, 0:S], ACT.Copy, scale=gm_t[:, t : t + 1])
-        for t in range(PACK):
-            nc.scalar.activation(z_all[:, t, :], ds[t][:], ACT.Copy, scale=gn_t[:, t : t + 1])
-        nc.scalar.activation(warm[:], odds[PACK - 1][:, S : S + 1], ACT.Abs_reciprocal_sqrt, scale=0.0, bias=1.0)
         z2_codes = sb.tile([P, S], U32, name="z2_codes", align_bytes=64)
         z2_scale = sb.tile([P, S], U8, name="z2_scale", align_bytes=64)
-        quantise("z2_woven", z2_all[:], z2_codes[:], z2_scale[:])
-        b_ps = product("hi", w3, w23_scale, 4, z2_codes, z2_scale)
         z_codes = sb.tile([P, S], U32, name="z_codes", align_bytes=64)
         z_scale = sb.tile([P, S], U8, name="z_scale", align_bytes=64)
-        quantise("z_woven", z_all[:], z_codes[:], z_scale[:])
-        a_ps = product("lo", w2, w23_scale, 0, z_codes, z_scale)
-
-        size = planes("size")
-        size2 = planes("size2")
-        for t in range(PACK):
-            nc.scalar.activation(size[t][:], b_ps[t][:], ACT.Abs)
-            nc.scalar.activation(size2[t][:], b_ps[t][:], ACT.Abs)
-        neg_a = planes("neg_a")
-        neg_a2 = planes("neg_a2")
-        for t in range(PACK):
-            nc.scalar.activation(neg_a[t][:], a_ps[t][:], ACT.Copy, scale=-1.0)
-            nc.sync.dma_start(neg_a2[t][:], neg_a[t][:])
-        den = planes("den")
-        for t in range(PACK):
-            for h in range(2):
-                nc.vector.tensor_tensor(den[t][:, cols(h)], size[t][:].indirect(half(n7_t, h)), size2[t][:, cols(h)], ALU.add)
-            nc.scalar.activation(den[t][:], den[t][:], ACT.Abs_reciprocal_sqrt, bias=0.5)
-            nc.scalar.activation(den[t][:], den[t][:], ACT.Square)
+        den = sb.tile([P, PACK, S], F32, name="den", align_bytes=64)
+        diff = sb.tile([P, PACK, S], F32, name="diff", align_bytes=64)
         out_codes = sb.tile([P, S], I32, name="out_codes", align_bytes=64)
         out_scale = sb.tile([P, S], U8, name="out_scale", align_bytes=64)
         out_rows = out_0.rearrange("(p t) c -> p t c", t=PACK)
         out_words = out_1[0].rearrange("p n r -> p (n r)").bitcast(I32)
-        for h in range(2):
-            diff = sb.tile([P, PACK, HALF], F32, name=f"diff{h}", align_bytes=64)
-            res = sb.tile([P, PACK, HALF], F32, name=f"res{h}", align_bytes=64)
-            for t in range(PACK):
-                nc.vector.tensor_tensor(diff[:, t, :], neg_a[t][:].indirect(half(n6_t, h)), neg_a2[t][:, cols(h)], ALU.subtract)
-            for t in range(PACK):
-                nc.vector.tensor_tensor(res[:, t, :], diff[:, t, :], den[t][:, cols(h)], ALU.mult)
-                if t % 2 == 1:
-                    nc.sync.dma_start(out_rows[:, t - 1 : t + 1, cols(h)], res[:, t - 1 : t + 1, :])
-            quantise(f"out_woven{h}", res[:], out_codes[:, cols(h)], out_scale[:, cols(h)])
-            nc.sync.dma_start(out_words[:, cols(h)], out_codes[:, cols(h)])
+
+        res = sb.tile([P, PACK, S], F32, name="res", align_bytes=64)
+
+        def join(t):
+            nc.vector.tensor_tensor(diff[:, t, :], neg_a[t][:].indirect(n6_t[:]), neg_a2[t][:], ALU.subtract)
+
+        def scale(t):
+            nc.vector.tensor_tensor(res[:, t, :], diff[:, t, :], den[:, t, :], ALU.mult)
+            nc.sync.dma_start(out_rows[:, t, :], res[:, t, :])
+
+        def finish():
+            woven = sb.tile([P, S, PACK], BF16, name="out_woven", align_bytes=64)
+            for h in range(2):
+                nc.vector.tensor_copy(woven[:, cols(h), :], res[:, :, cols(h)].rearrange("p t c -> p c t"))
+            for h in range(2):
+                nc.vector.quantize_mx(
+                    out=out_codes[:, cols(h)].bitcast(FP8X4), scales=out_scale[:, cols(h)],
+                    in_=woven[:, cols(h), :].rearrange("p c t -> p (c t)"),
+                )
+                nc.sync.dma_start(out_words[:, cols(h)], out_codes[:, cols(h)])
+
+        nc.scalar.copy(y[0][:, 0:S], y_ps[0][:])
+        nc.scalar.activation(ex[0][:, 0:S], y_ps[0][:], ACT.Exp, scale=0.5)
+        nc.sync.dma_start(e3[0][:], ex[0][:, 0:S])
+        nc.vector.tensor_copy(y[1][:, 0:S], y_ps[1][:])
+        nc.scalar.activation(e4[0][:, :], y[0][:].indirect(n4_t[:]), ACT.Exp, scale=0.5)
+        nc.scalar.activation(ex[1][:, 0:S], y_ps[1][:], ACT.Exp, scale=0.5)
+        nc.sync.dma_start(e3[1][:], ex[1][:, 0:S])
+        nc.scalar.copy(y[2][:, 0:S], y_ps[2][:])
+        nc.scalar.activation(e4[1][:, :], y[1][:].indirect(n4_t[:]), ACT.Exp, scale=0.5)
+        nc.scalar.activation(ex[2][:, 0:S], y_ps[2][:], ACT.Exp, scale=0.5)
+        nc.sync.dma_start(e3[2][:], ex[2][:, 0:S])
+        nc.scalar.copy(y[3][:, 0:S], y_ps[3][:])
+        nc.scalar.activation(e4[2][:, :], y[2][:].indirect(n4_t[:]), ACT.Exp, scale=0.5)
+        nc.scalar.activation(ex[3][:, 0:S], y_ps[3][:], ACT.Exp, scale=0.5)
+        nc.scalar.activation(e4[3][:, :], y[3][:].indirect(n4_t[:]), ACT.Exp, scale=0.5)
+        nc.scalar.activation(e3[3][:, :], y[3][:].indirect(n3_t[:]), ACT.Exp, scale=0.5)
+        nc.sync.dma_start(ds[0][:], y[0][:, 0:S])
+        nc.sync.dma_start(ds[1][:], y[1][:, 0:S])
+        nc.sync.dma_start(ds[2][:], y[2][:, 0:S])
+        nc.sync.dma_start(ds[3][:], y[3][:, 0:S])
+        gn_t = load_gain("gn_t", gn)
+        gm_t = load_gain("gm_t", gm)
+        n6_t = load_list("n6_t", n6)
+        n7_t = load_list("n7_t", n7)
+        load_scale_rows(nc.sync, w1s_raw, 4, w2_scales)
+        load_scale_rows(nc.sync, w1s_raw, 8, w3_scales)
+        nc.vector.tensor_tensor(odds[0][:, S : S + S], ex[0][:].indirect(n5_t[:]), e4[0][:, :], ALU.add)
+        nc.vector.tensor_tensor(odds[0][:, 0 : 0 + S], ex[0][:].indirect(n3_t[:]), e3[0][:, :], ALU.add)
+        nc.vector.tensor_tensor(odds[1][:, S : S + S], ex[1][:].indirect(n5_t[:]), e4[1][:, :], ALU.add)
+        nc.vector.tensor_tensor(odds[1][:, 0 : 0 + S], ex[1][:].indirect(n3_t[:]), e3[1][:, :], ALU.add)
+        nc.vector.tensor_tensor(odds[2][:, S : S + S], ex[2][:].indirect(n5_t[:]), e4[2][:, :], ALU.add)
+        nc.vector.tensor_tensor(odds[2][:, 0 : 0 + S], ex[2][:].indirect(n3_t[:]), e3[2][:, :], ALU.add)
+        nc.vector.tensor_tensor(odds[3][:, S : S + S], ex[3][:].indirect(n5_t[:]), e4[3][:, :], ALU.add)
+        nc.vector.tensor_tensor(odds[3][:, 0:S], ex[3][:, 0:S], e3[3][:], ALU.add)
+        nc.vector.tensor_copy(pa[0][:], y[0][:].indirect(n1_t[:]))
+        nc.scalar.activation(gate[0][:], y[0][:].indirect(n2_t[:]), ACT.Sigmoid)
+        nc.vector.tensor_copy(pa[1][:], y[1][:].indirect(n1_t[:]))
+        nc.scalar.activation(gate[1][:], y[1][:].indirect(n2_t[:]), ACT.Sigmoid)
+        nc.vector.tensor_copy(pa[2][:], y[2][:].indirect(n1_t[:]))
+        nc.scalar.activation(gate[2][:], y[2][:].indirect(n2_t[:]), ACT.Sigmoid)
+        nc.vector.tensor_copy(pa[3][:], y[3][:].indirect(n1_t[:]))
+        nc.scalar.activation(gate[3][:], y[3][:].indirect(n2_t[:]), ACT.Sigmoid)
+        w2 = deal("w2", w2_raw, I32, nc.vector)
+        w3 = deal("w3", w3_raw, I32, nc.vector)
+        w23_scale = deal("w23_scale", w1s_raw, U8, nc.gpsimd)
+        nc.scalar.activation(odds[0][:], odds[0][:], ACT.Ln)
+        nc.scalar.activation(odds[1][:], odds[1][:], ACT.Ln)
+        nc.scalar.activation(odds[2][:], odds[2][:], ACT.Ln)
+        nc.scalar.activation(odds[3][:], odds[3][:], ACT.Ln)
+        nc.vector.tensor_tensor(ds[0][:].indirect(n2_t[:]), pa[0][:], gate[0][:], ALU.mult)
+        nc.vector.tensor_tensor(ds[1][:].indirect(n2_t[:]), pa[1][:], gate[1][:], ALU.mult)
+        nc.vector.tensor_tensor(ds[2][:].indirect(n2_t[:]), pa[2][:], gate[2][:], ALU.mult)
+        nc.vector.tensor_tensor(ds[3][:].indirect(n2_t[:]), pa[3][:], gate[3][:], ALU.mult)
+        nc.vector.tensor_tensor(odds[0][:, 0:S], odds[0][:, 0:S], odds[0][:, S : 2 * S], ALU.subtract)
+        nc.vector.tensor_tensor(odds[1][:, 0:S], odds[1][:, 0:S], odds[1][:, S : 2 * S], ALU.subtract)
+        nc.vector.tensor_tensor(odds[2][:, 0:S], odds[2][:, 0:S], odds[2][:, S : 2 * S], ALU.subtract)
+        nc.vector.tensor_tensor(odds[3][:, 0:S], odds[3][:, 0:S], odds[3][:, S : 2 * S], ALU.subtract)
+        nc.scalar.activation(z2_all[:, 0, :], odds[0][:, 0:S], ACT.Copy, scale=gm_t[:, 0 : 1])
+        nc.scalar.activation(z2_all[:, 1, :], odds[1][:, 0:S], ACT.Copy, scale=gm_t[:, 1 : 2])
+        nc.scalar.activation(z2_all[:, 2, :], odds[2][:, 0:S], ACT.Copy, scale=gm_t[:, 2 : 3])
+        nc.vector.tensor_scalar(z2_all[:, 3, :], odds[3][:, 0:S], gm_t[:, 3 : 4], None, ALU.mult)
+        nc.scalar.activation(z_all[:, 0, :], ds[0][:], ACT.Copy, scale=gn_t[:, 0 : 1])
+        nc.scalar.activation(z_all[:, 1, :], ds[1][:], ACT.Copy, scale=gn_t[:, 1 : 2])
+        nc.scalar.activation(z_all[:, 2, :], ds[2][:], ACT.Copy, scale=gn_t[:, 2 : 3])
+        nc.scalar.activation(z_all[:, 3, :], ds[3][:], ACT.Copy, scale=gn_t[:, 3 : 4])
+        quantise("z2_woven", z2_all[:], z2_codes[:], z2_scale[:])
+        b_ps = product("hi", w3, w23_scale, 8, z2_codes, z2_scale)
+        quantise("z_woven", z_all[:], z_codes[:], z_scale[:])
+        a_ps = product("lo", w2, w23_scale, 4, z_codes, z_scale)
+        nc.scalar.activation(size[0][:, 0:S], b_ps[0][:], ACT.Abs)
+        nc.scalar.activation(size2[0][:], b_ps[0][:], ACT.Abs)
+        nc.scalar.activation(size[1][:, 0:S], b_ps[1][:], ACT.Abs)
+        nc.scalar.activation(size2[1][:], b_ps[1][:], ACT.Abs)
+        nc.scalar.activation(neg_a[0][:, 0:S], a_ps[0][:], ACT.Copy, scale=-1.0)
+        nc.sync.dma_start(neg_a2[0][:], neg_a[0][:, 0:S])
+        nc.scalar.activation(size[2][:, 0:S], b_ps[2][:], ACT.Abs)
+        nc.scalar.activation(size2[2][:], b_ps[2][:], ACT.Abs)
+        nc.scalar.activation(neg_a[1][:, 0:S], a_ps[1][:], ACT.Copy, scale=-1.0)
+        nc.sync.dma_start(neg_a2[1][:], neg_a[1][:, 0:S])
+        nc.scalar.activation(size[3][:, 0:S], b_ps[3][:], ACT.Abs)
+        nc.scalar.activation(size2[3][:], b_ps[3][:], ACT.Abs)
+        nc.scalar.activation(neg_a[2][:, 0:S], a_ps[2][:], ACT.Copy, scale=-1.0)
+        nc.sync.dma_start(neg_a2[2][:], neg_a[2][:, 0:S])
+        nc.scalar.activation(neg_a[3][:, 0:S], a_ps[3][:], ACT.Copy, scale=-1.0)
+        nc.sync.dma_start(neg_a2[3][:], neg_a[3][:, 0:S])
+        nc.vector.tensor_tensor(den[:, 0, :], size[0][:].indirect(n7_t[:]), size2[0][:, :], ALU.add)
+        nc.scalar.activation(den[:, 0, :], den[:, 0, :], ACT.Abs_reciprocal_sqrt, bias=0.5)
+        nc.scalar.activation(den[:, 0, :], den[:, 0, :], ACT.Square)
+        nc.vector.tensor_tensor(den[:, 1, :], size[1][:].indirect(n7_t[:]), size2[1][:, :], ALU.add)
+        nc.scalar.activation(den[:, 1, :], den[:, 1, :], ACT.Abs_reciprocal_sqrt, bias=0.5)
+        nc.scalar.activation(den[:, 1, :], den[:, 1, :], ACT.Square)
+        nc.vector.tensor_tensor(den[:, 2, :], size[2][:].indirect(n7_t[:]), size2[2][:, :], ALU.add)
+        nc.scalar.activation(den[:, 2, :], den[:, 2, :], ACT.Abs_reciprocal_sqrt, bias=0.5)
+        nc.scalar.activation(den[:, 2, :], den[:, 2, :], ACT.Square)
+        nc.vector.tensor_tensor(den[:, 3, :], size[3][:].indirect(n7_t[:]), size2[3][:, :], ALU.add)
+        nc.scalar.activation(den[:, 3, :], den[:, 3, :], ACT.Abs_reciprocal_sqrt, bias=0.5)
+        nc.scalar.activation(den[:, 3, :], den[:, 3, :], ACT.Square)
+        join(0)
+        join(1)
+        scale(0)
+        join(2)
+        scale(1)
+        join(3)
+        scale(2)
+        scale(3)
+        finish()
         for q in range(4):
             queue = nc.sync if q % 2 == 0 else nc.scalar
             queue.dma_start(

@@ -83,24 +83,34 @@ def tile_picked_forknormbfoldodds_none_po_kernel(
                 banks.append(bank)
             return banks
 
-        def quantise(name, src, codes, scale):
-            width = src.shape[2]
-            woven = sb.tile([P, width, PACK], BF16, name=name, align_bytes=64)
-            nc.vector.tensor_copy(woven[:], src.rearrange("p t c -> p c t"))
-            nc.vector.quantize_mx(
-                out=codes.bitcast(FP8X4), scales=scale, in_=woven[:].rearrange("p c t -> p (c t)")
-            )
+        def quantise(name, src, codes, scale, paired=False):
+            woven = sb.tile([P, S, PACK], BF16, name=name, align_bytes=64)
+            for h in range(2):
+                if paired:
+                    nc.vector.tensor_copy(
+                        woven[:].rearrange("p c t -> p (c t)").bitcast(I32).rearrange("p (c u) -> p c u", u=2)[:, cols(h), :],
+                        src.rearrange("p u c e -> p u (c e)").bitcast(I32)[:, :, cols(h)].rearrange("p u c -> p c u"),
+                    )
+                else:
+                    nc.vector.tensor_copy(
+                    woven[:, cols(h), :].rearrange("p (c i) t -> p c t i", i=4), src[:, :, cols(h)].rearrange("p t (c i) -> p c t i", i=4)
+                )
+            for h in range(2):
+                nc.vector.quantize_mx(
+                    out=codes[:, cols(h)].bitcast(FP8X4), scales=scale[:, cols(h)],
+                    in_=woven[:, cols(h), :].rearrange("p c t -> p (c t)"),
+                )
 
         xs_raw = sb.tile([P, T], U8, name="xs_raw", align_bytes=64)
         w1s_raw = sb.tile([P, S], U8, name="w1s_raw", align_bytes=64)
         nc.vector.memset(xs_raw[:].bitcast(I32), 0)
         nc.vector.memset(w1s_raw[:].bitcast(I32), 0)
-        load_scale_rows(nc.sync, xs_raw, 0, x_scales)
+        load_scale_rows(nc.scalar, xs_raw, 0, x_scales)
         w1_raw = load_words("w1_raw", w1_words)
         offs_t = load_list("offs_t", offs)
+        n4_t = load_list("n4_t", n4)
         xw_raw = load_words("xw_raw", x_words)
         load_scale_rows(nc.sync, w1s_raw, 0, w1_scales)
-        n4_t = load_list("n4_t", n4)
         w2_raw = load_words("w2_raw", w2_words)
         w3_raw = load_words("w3_raw", w3_words)
         n1_t = load_list("n1_t", n1)
@@ -153,7 +163,9 @@ def tile_picked_forknormbfoldodds_none_po_kernel(
         def finish():
             woven = sb.tile([P, S, PACK], BF16, name="out_woven", align_bytes=64)
             for h in range(2):
-                nc.vector.tensor_copy(woven[:, cols(h), :], res[:, :, cols(h)].rearrange("p t c -> p c t"))
+                nc.vector.tensor_copy(
+                    woven[:, cols(h), :].rearrange("p (c i) t -> p c t i", i=4), res[:, :, cols(h)].rearrange("p t (c i) -> p c t i", i=4)
+                )
             for h in range(2):
                 nc.vector.quantize_mx(
                     out=out_codes[:, cols(h)].bitcast(FP8X4), scales=out_scale[:, cols(h)],

@@ -1,6 +1,7 @@
 from contextlib import ExitStack
 
 import concourse.mybir as mybir
+from concourse.masks import make_identity
 
 F32 = mybir.dt.float32
 BF16 = mybir.dt.bfloat16
@@ -18,7 +19,7 @@ T = 2048
 S = 512
 HALF = S // 2
 LIST_HALF = HALF // 16
-SCALAR_N3 = 1
+SCALAR_N3 = 4
 
 FLOPS = 3 * 2 * 512 * 512 * 512
 
@@ -92,9 +93,7 @@ def tile_picked_forknormbfoldodds_none_po_kernel(
                         src.rearrange("p u c e -> p u (c e)").bitcast(I32)[:, :, cols(h)].rearrange("p u c -> p c u"),
                     )
                 else:
-                    nc.vector.tensor_copy(
-                    woven[:, cols(h), :].rearrange("p (c i) t -> p c t i", i=4), src[:, :, cols(h)].rearrange("p t (c i) -> p c t i", i=4)
-                )
+                    nc.vector.tensor_copy(woven[:, cols(h), :], src[:, :, cols(h)].rearrange("p t c -> p c t"))
             for h in range(2):
                 nc.vector.quantize_mx(
                     out=codes[:, cols(h)].bitcast(FP8X4), scales=scale[:, cols(h)],
@@ -105,17 +104,17 @@ def tile_picked_forknormbfoldodds_none_po_kernel(
         w1s_raw = sb.tile([P, S], U8, name="w1s_raw", align_bytes=64)
         nc.vector.memset(xs_raw[:].bitcast(I32), 0)
         nc.vector.memset(w1s_raw[:].bitcast(I32), 0)
-        load_scale_rows(nc.scalar, xs_raw, 0, x_scales)
+        load_scale_rows(nc.sync, xs_raw, 0, x_scales)
         w1_raw = load_words("w1_raw", w1_words)
         offs_t = load_list("offs_t", offs)
-        n4_t = load_list("n4_t", n4)
         xw_raw = load_words("xw_raw", x_words)
         load_scale_rows(nc.sync, w1s_raw, 0, w1_scales)
+        n4_t = load_list("n4_t", n4)
+        n3_t = load_list("n3_t", n3)
         w2_raw = load_words("w2_raw", w2_words)
+        n5_t = load_list("n5_t", n5)
         w3_raw = load_words("w3_raw", w3_words)
         n1_t = load_list("n1_t", n1)
-        n5_t = load_list("n5_t", n5)
-        n3_t = load_list("n3_t", n3)
         n2_t = load_list("n2_t", n2)
 
         w1_scale = deal("w1_scale", w1s_raw, U8, nc.gpsimd)
@@ -136,9 +135,7 @@ def tile_picked_forknormbfoldodds_none_po_kernel(
         odds = planes("odds", 2 * S)
         pa = planes("pa", HALF)
         gate = planes("gate", HALF)
-        size2 = planes("size2")
         neg_a2 = planes("neg_a2")
-        z2_all = sb.tile([P, PACK, S], BF16, name="z2_all", align_bytes=64)
         z_all = sb.tile([P, PACK, S], BF16, name="z_all", align_bytes=64)
         z2_codes = sb.tile([P, S], U32, name="z2_codes", align_bytes=64)
         z2_scale = sb.tile([P, S], U8, name="z2_scale", align_bytes=64)
@@ -157,15 +154,14 @@ def tile_picked_forknormbfoldodds_none_po_kernel(
             nc.vector.tensor_tensor(diff[:, t, :], neg_a[t][:].indirect(n6_t[:]), neg_a2[t][:], ALU.subtract)
 
         def scale(t):
-            nc.vector.tensor_tensor(res[:, t, :], diff[:, t, :], den[:, t, :], ALU.mult)
+            nc.vector.tensor_tensor(res[:, t, :], recip[t][:].rearrange("p j c -> p (j c)"), diff[:, t, :], ALU.mult)
             nc.sync.dma_start(out_rows[:, t, :], res[:, t, :])
 
         def finish():
             woven = sb.tile([P, S, PACK], BF16, name="out_woven", align_bytes=64)
+            nc.scalar.copy(woven[:, :, 0:2], res[:, 0:2, :].rearrange("p t c -> p c t"))
             for h in range(2):
-                nc.vector.tensor_copy(
-                    woven[:, cols(h), :].rearrange("p (c i) t -> p c t i", i=4), res[:, :, cols(h)].rearrange("p t (c i) -> p c t i", i=4)
-                )
+                nc.vector.tensor_copy(woven[:, cols(h), 2:4], res[:, 2:4, cols(h)].rearrange("p t c -> p c t"))
             for h in range(2):
                 nc.vector.quantize_mx(
                     out=out_codes[:, cols(h)].bitcast(FP8X4), scales=out_scale[:, cols(h)],
@@ -173,22 +169,38 @@ def tile_picked_forknormbfoldodds_none_po_kernel(
                 )
                 nc.sync.dma_start(out_words[:, cols(h)], out_codes[:, cols(h)])
 
-        nc.scalar.copy(y[0][:, 0:S], y_ps[0][:])
+        ident = sb.tile([P, P], F32, name="ident")
+        make_identity(nc, ident[:])
+        e5 = planes("e5")
+        g7 = planes("g7")
+
+        def bank(name):
+            return ps.tile([P, PACK, P], F32, name=name, tag=name)
+
+        def turn(dst, *srcs):
+            for i, src in enumerate(srcs):
+                nc.tensor.matmul(dst, lhsT=src, rhs=ident[:], start=i == 0, stop=i == len(srcs) - 1, is_transpose=True)
+
+        def turned_sum(name, first, second):
+            dst = bank(name)
+            for j in range(PACK):
+                turn(dst[:, j, :], first[:, j * P : (j + 1) * P], second[:, j * P : (j + 1) * P])
+            return dst[:].rearrange("c j p -> c (j p)")
+
         nc.scalar.activation(ex[0][:, 0:S], y_ps[0][:], ACT.Exp, scale=0.5)
-        nc.sync.dma_start(e3[0][:], ex[0][:, 0:S])
-        nc.vector.tensor_copy(y[1][:, 0:S], y_ps[1][:])
-        nc.scalar.activation(e4[0][:, :], y[0][:].indirect(n4_t[:]), ACT.Exp, scale=0.5)
+        nc.scalar.copy(y[0][:, 0:S], y_ps[0][:])
         nc.scalar.activation(ex[1][:, 0:S], y_ps[1][:], ACT.Exp, scale=0.5)
-        nc.sync.dma_start(e3[1][:], ex[1][:, 0:S])
-        nc.scalar.copy(y[2][:, 0:S], y_ps[2][:])
-        nc.scalar.activation(e4[1][:, :], y[1][:].indirect(n4_t[:]), ACT.Exp, scale=0.5)
+        nc.scalar.activation(e4[0][:], y[0][:].indirect(n4_t[:]), ACT.Exp, scale=0.5)
+        nc.scalar.copy(y[1][:, 0:S], y_ps[1][:])
         nc.scalar.activation(ex[2][:, 0:S], y_ps[2][:], ACT.Exp, scale=0.5)
-        nc.sync.dma_start(e3[2][:], ex[2][:, 0:S])
+        nc.scalar.activation(e4[1][:], y[1][:].indirect(n4_t[:]), ACT.Exp, scale=0.5)
+        nc.scalar.copy(y[2][:, 0:S], y_ps[2][:])
+        nc.scalar.activation(e4[2][:], y[2][:].indirect(n4_t[:]), ACT.Exp, scale=0.5)
         nc.scalar.copy(y[3][:, 0:S], y_ps[3][:])
-        nc.scalar.activation(e4[2][:, :], y[2][:].indirect(n4_t[:]), ACT.Exp, scale=0.5)
         nc.scalar.activation(ex[3][:, 0:S], y_ps[3][:], ACT.Exp, scale=0.5)
-        nc.scalar.activation(e4[3][:, :], y[3][:].indirect(n4_t[:]), ACT.Exp, scale=0.5)
-        nc.scalar.activation(e3[3][:, :], y[3][:].indirect(n3_t[:]), ACT.Exp, scale=0.5)
+        nc.scalar.activation(e4[3][:], y[3][:].indirect(n4_t[:]), ACT.Exp, scale=0.5)
+        load_scale_rows(nc.sync, w1s_raw, 4, w2_scales)
+        load_scale_rows(nc.sync, w1s_raw, 8, w3_scales)
         nc.sync.dma_start(ds[0][:], y[0][:, 0:S])
         nc.sync.dma_start(ds[1][:], y[1][:, 0:S])
         nc.sync.dma_start(ds[2][:], y[2][:, 0:S])
@@ -197,85 +209,118 @@ def tile_picked_forknormbfoldodds_none_po_kernel(
         gm_t = load_gain("gm_t", gm)
         n6_t = load_list("n6_t", n6)
         n7_t = load_list("n7_t", n7)
-        load_scale_rows(nc.sync, w1s_raw, 4, w2_scales)
-        load_scale_rows(nc.sync, w1s_raw, 8, w3_scales)
-        nc.vector.tensor_tensor(odds[0][:, S : S + S], ex[0][:].indirect(n5_t[:]), e4[0][:, :], ALU.add)
-        nc.vector.tensor_tensor(odds[0][:, 0 : 0 + S], ex[0][:].indirect(n3_t[:]), e3[0][:, :], ALU.add)
-        nc.vector.tensor_tensor(odds[1][:, S : S + S], ex[1][:].indirect(n5_t[:]), e4[1][:, :], ALU.add)
-        nc.vector.tensor_tensor(odds[1][:, 0 : 0 + S], ex[1][:].indirect(n3_t[:]), e3[1][:, :], ALU.add)
-        nc.vector.tensor_tensor(odds[2][:, S : S + S], ex[2][:].indirect(n5_t[:]), e4[2][:, :], ALU.add)
-        nc.vector.tensor_tensor(odds[2][:, 0 : 0 + S], ex[2][:].indirect(n3_t[:]), e3[2][:, :], ALU.add)
-        nc.vector.tensor_tensor(odds[3][:, S : S + S], ex[3][:].indirect(n5_t[:]), e4[3][:, :], ALU.add)
-        nc.vector.tensor_tensor(odds[3][:, 0:S], ex[3][:, 0:S], e3[3][:], ALU.add)
+        nc.vector.tensor_copy(e3[0][:], ex[0][:].indirect(n3_t[:]))
+        nc.vector.tensor_copy(e5[0][:], ex[0][:].indirect(n5_t[:]))
         nc.vector.tensor_copy(pa[0][:], y[0][:].indirect(n1_t[:]))
-        nc.scalar.activation(gate[0][:], y[0][:].indirect(n2_t[:]), ACT.Sigmoid)
+        nc.vector.tensor_copy(e3[1][:], ex[1][:].indirect(n3_t[:]))
+        nc.vector.tensor_copy(e5[1][:], ex[1][:].indirect(n5_t[:]))
         nc.vector.tensor_copy(pa[1][:], y[1][:].indirect(n1_t[:]))
-        nc.scalar.activation(gate[1][:], y[1][:].indirect(n2_t[:]), ACT.Sigmoid)
+        nc.vector.tensor_copy(e3[2][:], ex[2][:].indirect(n3_t[:]))
+        nc.vector.tensor_copy(e5[2][:], ex[2][:].indirect(n5_t[:]))
         nc.vector.tensor_copy(pa[2][:], y[2][:].indirect(n1_t[:]))
-        nc.scalar.activation(gate[2][:], y[2][:].indirect(n2_t[:]), ACT.Sigmoid)
+        nc.vector.tensor_copy(e3[3][:], ex[3][:].indirect(n3_t[:]))
+        nc.vector.tensor_copy(e5[3][:], ex[3][:].indirect(n5_t[:]))
         nc.vector.tensor_copy(pa[3][:], y[3][:].indirect(n1_t[:]))
+        nc.scalar.activation(gate[0][:], y[0][:].indirect(n2_t[:]), ACT.Sigmoid)
+        nc.scalar.activation(gate[1][:], y[1][:].indirect(n2_t[:]), ACT.Sigmoid)
+        nc.scalar.activation(gate[2][:], y[2][:].indirect(n2_t[:]), ACT.Sigmoid)
         nc.scalar.activation(gate[3][:], y[3][:].indirect(n2_t[:]), ACT.Sigmoid)
         w2 = deal("w2", w2_raw, I32, nc.vector)
         w3 = deal("w3", w3_raw, I32, nc.vector)
         w23_scale = deal("w23_scale", w1s_raw, U8, nc.gpsimd)
-        nc.scalar.activation(odds[0][:], odds[0][:], ACT.Ln)
-        nc.scalar.activation(odds[1][:], odds[1][:], ACT.Ln)
-        nc.scalar.activation(odds[2][:], odds[2][:], ACT.Ln)
-        nc.scalar.activation(odds[3][:], odds[3][:], ACT.Ln)
+        below = turned_sum("hi0", e4[0][:], e5[0][:])
+        above = turned_sum("hi1", ex[0][:, 0:S], e3[0][:])
+        nc.scalar.activation(odds[0][:, S : 2 * S], below, ACT.Ln)
+        nc.gpsimd.tensor_scalar(odds[0][:, S : 2 * S], odds[0][:, S : 2 * S], -1.0, 0.0, ALU.mult, ALU.add)
+        nc.scalar.activation(odds[0][:, 0:S], above, ACT.Ln)
+        below = turned_sum("hi2", e4[1][:], e5[1][:])
+        above = turned_sum("hi3", ex[1][:, 0:S], e3[1][:])
+        nc.scalar.activation(odds[1][:, S : 2 * S], below, ACT.Ln)
+        nc.gpsimd.tensor_scalar(odds[1][:, S : 2 * S], odds[1][:, S : 2 * S], -1.0, 0.0, ALU.mult, ALU.add)
+        nc.scalar.activation(odds[1][:, 0:S], above, ACT.Ln)
+        below = turned_sum("lo0", e4[2][:], e5[2][:])
+        above = turned_sum("lo1", ex[2][:, 0:S], e3[2][:])
+        nc.scalar.activation(odds[2][:, S : 2 * S], below, ACT.Ln)
+        nc.gpsimd.tensor_scalar(odds[2][:, S : 2 * S], odds[2][:, S : 2 * S], -1.0, 0.0, ALU.mult, ALU.add)
+        nc.scalar.activation(odds[2][:, 0:S], above, ACT.Ln)
+        below = turned_sum("lo2", e4[3][:], e5[3][:])
+        above = turned_sum("lo3", ex[3][:, 0:S], e3[3][:])
+        nc.scalar.activation(odds[3][:, S : 2 * S], below, ACT.Ln)
+        nc.gpsimd.tensor_scalar(odds[3][:, S : 2 * S], odds[3][:, S : 2 * S], -1.0, 0.0, ALU.mult, ALU.add)
+        nc.scalar.activation(odds[3][:, 0:S], above, ACT.Ln)
         nc.vector.tensor_tensor(ds[0][:].indirect(n2_t[:]), pa[0][:], gate[0][:], ALU.mult)
         nc.vector.tensor_tensor(ds[1][:].indirect(n2_t[:]), pa[1][:], gate[1][:], ALU.mult)
         nc.vector.tensor_tensor(ds[2][:].indirect(n2_t[:]), pa[2][:], gate[2][:], ALU.mult)
         nc.vector.tensor_tensor(ds[3][:].indirect(n2_t[:]), pa[3][:], gate[3][:], ALU.mult)
-        nc.vector.tensor_tensor(odds[0][:, 0:S], odds[0][:, 0:S], odds[0][:, S : 2 * S], ALU.subtract)
-        nc.vector.tensor_tensor(odds[1][:, 0:S], odds[1][:, 0:S], odds[1][:, S : 2 * S], ALU.subtract)
-        nc.vector.tensor_tensor(odds[2][:, 0:S], odds[2][:, 0:S], odds[2][:, S : 2 * S], ALU.subtract)
-        nc.vector.tensor_tensor(odds[3][:, 0:S], odds[3][:, 0:S], odds[3][:, S : 2 * S], ALU.subtract)
-        nc.scalar.activation(z2_all[:, 0, :], odds[0][:, 0:S], ACT.Copy, scale=gm_t[:, 0 : 1])
-        nc.scalar.activation(z2_all[:, 1, :], odds[1][:, 0:S], ACT.Copy, scale=gm_t[:, 1 : 2])
-        nc.scalar.activation(z2_all[:, 2, :], odds[2][:, 0:S], ACT.Copy, scale=gm_t[:, 2 : 3])
-        nc.vector.tensor_scalar(z2_all[:, 3, :], odds[3][:, 0:S], gm_t[:, 3 : 4], None, ALU.mult)
         nc.scalar.activation(z_all[:, 0, :], ds[0][:], ACT.Copy, scale=gn_t[:, 0 : 1])
         nc.scalar.activation(z_all[:, 1, :], ds[1][:], ACT.Copy, scale=gn_t[:, 1 : 2])
         nc.scalar.activation(z_all[:, 2, :], ds[2][:], ACT.Copy, scale=gn_t[:, 2 : 3])
         nc.scalar.activation(z_all[:, 3, :], ds[3][:], ACT.Copy, scale=gn_t[:, 3 : 4])
-        quantise("z2_woven", z2_all[:], z2_codes[:], z2_scale[:])
-        b_ps = product("hi", w3, w23_scale, 8, z2_codes, z2_scale)
+        back = [bank(f"hi{j}") for j in range(PACK)]
+        for t in range(PACK):
+            for j in range(PACK):
+                turn(back[j][:, t, :], odds[t][:, j * P : (j + 1) * P], odds[t][:, S + j * P : S + (j + 1) * P])
+        z2_woven = sb.tile([P, S, PACK], BF16, name="z2_woven", align_bytes=64)
+        for j in range(PACK):
+            nc.vector.tensor_tensor(
+                z2_woven[:, j * P : (j + 1) * P, :], back[j][:].rearrange("p t c -> p c t"),
+                gm_t[:].unsqueeze(1).to_broadcast([P, P, PACK]), ALU.mult,
+            )
+        for h in range(2):
+            nc.vector.quantize_mx(
+                out=z2_codes[:, cols(h)].bitcast(FP8X4), scales=z2_scale[:, cols(h)],
+                in_=z2_woven[:, cols(h), :].rearrange("p c t -> p (c t)"),
+            )
+        b_ps = product("lo", w3, w23_scale, 8, z2_codes, z2_scale)
         quantise("z_woven", z_all[:], z_codes[:], z_scale[:])
-        a_ps = product("lo", w2, w23_scale, 4, z_codes, z_scale)
+        a_ps = product("hi", w2, w23_scale, 4, z_codes, z_scale)
         nc.scalar.activation(size[0][:, 0:S], b_ps[0][:], ACT.Abs)
-        nc.scalar.activation(size2[0][:], b_ps[0][:], ACT.Abs)
         nc.scalar.activation(size[1][:, 0:S], b_ps[1][:], ACT.Abs)
-        nc.scalar.activation(size2[1][:], b_ps[1][:], ACT.Abs)
         nc.scalar.activation(neg_a[0][:, 0:S], a_ps[0][:], ACT.Copy, scale=-1.0)
         nc.sync.dma_start(neg_a2[0][:], neg_a[0][:, 0:S])
         nc.scalar.activation(size[2][:, 0:S], b_ps[2][:], ACT.Abs)
-        nc.scalar.activation(size2[2][:], b_ps[2][:], ACT.Abs)
         nc.scalar.activation(neg_a[1][:, 0:S], a_ps[1][:], ACT.Copy, scale=-1.0)
         nc.sync.dma_start(neg_a2[1][:], neg_a[1][:, 0:S])
         nc.scalar.activation(size[3][:, 0:S], b_ps[3][:], ACT.Abs)
-        nc.scalar.activation(size2[3][:], b_ps[3][:], ACT.Abs)
         nc.scalar.activation(neg_a[2][:, 0:S], a_ps[2][:], ACT.Copy, scale=-1.0)
         nc.sync.dma_start(neg_a2[2][:], neg_a[2][:, 0:S])
         nc.scalar.activation(neg_a[3][:, 0:S], a_ps[3][:], ACT.Copy, scale=-1.0)
         nc.sync.dma_start(neg_a2[3][:], neg_a[3][:, 0:S])
-        nc.vector.tensor_tensor(den[:, 0, :], size[0][:].indirect(n7_t[:]), size2[0][:, :], ALU.add)
-        nc.scalar.activation(den[:, 0, :], den[:, 0, :], ACT.Abs_reciprocal_sqrt, bias=0.5)
+        nc.vector.tensor_copy(g7[0][:], size[0][:].indirect(n7_t[:]))
+        nc.vector.tensor_copy(g7[1][:], size[1][:].indirect(n7_t[:]))
+        nc.vector.tensor_copy(g7[2][:], size[2][:].indirect(n7_t[:]))
+        nc.vector.tensor_copy(g7[3][:], size[3][:].indirect(n7_t[:]))
+        recip = []
+        total = turned_sum("lo0", size[0][:, 0:S], g7[0][:])
+        nc.scalar.activation(den[:, 0, :], total, ACT.Abs_reciprocal_sqrt, bias=0.5)
+        total = turned_sum("lo1", size[1][:, 0:S], g7[1][:])
+        nc.scalar.activation(den[:, 1, :], total, ACT.Abs_reciprocal_sqrt, bias=0.5)
+        total = turned_sum("lo2", size[2][:, 0:S], g7[2][:])
+        nc.scalar.activation(den[:, 2, :], total, ACT.Abs_reciprocal_sqrt, bias=0.5)
+        total = turned_sum("lo3", size[3][:, 0:S], g7[3][:])
+        nc.scalar.activation(den[:, 3, :], total, ACT.Abs_reciprocal_sqrt, bias=0.5)
         nc.scalar.activation(den[:, 0, :], den[:, 0, :], ACT.Square)
-        nc.vector.tensor_tensor(den[:, 1, :], size[1][:].indirect(n7_t[:]), size2[1][:, :], ALU.add)
-        nc.scalar.activation(den[:, 1, :], den[:, 1, :], ACT.Abs_reciprocal_sqrt, bias=0.5)
+        recip.append(bank("hi0"))
+        for j in range(PACK):
+            turn(recip[0][:, j, :], den[:, 0, j * P : (j + 1) * P])
         nc.scalar.activation(den[:, 1, :], den[:, 1, :], ACT.Square)
-        nc.vector.tensor_tensor(den[:, 2, :], size[2][:].indirect(n7_t[:]), size2[2][:, :], ALU.add)
-        nc.scalar.activation(den[:, 2, :], den[:, 2, :], ACT.Abs_reciprocal_sqrt, bias=0.5)
+        recip.append(bank("hi1"))
+        for j in range(PACK):
+            turn(recip[1][:, j, :], den[:, 1, j * P : (j + 1) * P])
         nc.scalar.activation(den[:, 2, :], den[:, 2, :], ACT.Square)
-        nc.vector.tensor_tensor(den[:, 3, :], size[3][:].indirect(n7_t[:]), size2[3][:, :], ALU.add)
-        nc.scalar.activation(den[:, 3, :], den[:, 3, :], ACT.Abs_reciprocal_sqrt, bias=0.5)
+        recip.append(bank("hi2"))
+        for j in range(PACK):
+            turn(recip[2][:, j, :], den[:, 2, j * P : (j + 1) * P])
         nc.scalar.activation(den[:, 3, :], den[:, 3, :], ACT.Square)
+        recip.append(bank("hi3"))
+        for j in range(PACK):
+            turn(recip[3][:, j, :], den[:, 3, j * P : (j + 1) * P])
         join(0)
         join(1)
-        scale(0)
         join(2)
-        scale(1)
+        scale(0)
         join(3)
+        scale(1)
         scale(2)
         scale(3)
         finish()

@@ -15,13 +15,16 @@ ALU = mybir.AluOpType
 
 P = 128
 PACK = 4
+QUADRANTS = 4
 T = 2048
 S = 512
+BLOCKS = S // P
 HALF = S // 2
-LIST_HALF = HALF // 16
-SCALAR_N3 = 4
+WINDOW = 2 * S
+SCALAR_N4 = 3
+W2_ROW, W3_ROW = 4, 8
 
-FLOPS = 3 * 2 * 512 * 512 * 512
+FLOPS = 3 * 2 * S * S * S
 
 
 def tile_picked_forknormbfoldodds_none_po_kernel(
@@ -36,6 +39,15 @@ def tile_picked_forknormbfoldodds_none_po_kernel(
         def planes(name, width=S):
             return [sb.tile([P, width], F32, name=f"{name}{t}", align_bytes=64) for t in range(PACK)]
 
+        def bank(index):
+            return ps.tile([P, S], F32, name=f"bank{index}", tag=f"bank{index}")
+
+        def block(j):
+            return slice(j * P, (j + 1) * P)
+
+        def half(h):
+            return slice(h * HALF, (h + 1) * HALF)
+
         def load_list(name, src):
             tile = sb.tile(list(src.shape), U16, name=name)
             nc.sync.dma_start(tile[:], src)
@@ -46,9 +58,9 @@ def tile_picked_forknormbfoldodds_none_po_kernel(
             nc.sync.dma_start(tile[:], src[0].rearrange("p n r -> p (n r)").bitcast(I32))
             return tile
 
-        def load_scale_rows(queue, tile, first, src):
-            for q in range(4):
-                queue.dma_start(
+        def load_scale_rows(tile, first, src):
+            for q in range(QUADRANTS):
+                nc.sync.dma_start(
                     tile[32 * q + first : 32 * q + first + 4, :].bitcast(I32),
                     src[0, 4 * q : 4 * q + 4, :].bitcast(I32),
                 )
@@ -66,49 +78,51 @@ def tile_picked_forknormbfoldodds_none_po_kernel(
             )
             return tile
 
-        def half(offsets, h):
-            return offsets[:, h * LIST_HALF : (h + 1) * LIST_HALF]
-
-        def cols(h):
-            return slice(h * HALF, (h + 1) * HALF)
-
-        def product(tag, w, w_scale, first, codes, scale):
-            banks = []
+        def product(first_bank, w, w_scale, first_row, codes, scale):
+            result = []
             for t in range(PACK):
-                bank = ps.tile([P, S], F32, name=f"{tag}{t}", tag=f"{tag}{t}")
-                m = slice(t * P, (t + 1) * P)
+                plane = bank(first_bank + t)
                 nc.tensor.matmul_mx(
-                    out=bank[:], lhsT=w[:, m].bitcast(FP8X4), lhsT_scale=w_scale[first:P, m],
+                    out=plane[:], lhsT=w[:, block(t)].bitcast(FP8X4), lhsT_scale=w_scale[first_row:P, block(t)],
                     rhs=codes[:].bitcast(FP8X4), rhs_scale=scale[:], start=True, stop=True,
                 )
-                banks.append(bank)
-            return banks
+                result.append(plane)
+            return result
 
-        def quantise(name, src, codes, scale, paired=False):
-            woven = sb.tile([P, S, PACK], BF16, name=name, align_bytes=64)
-            for h in range(2):
-                if paired:
-                    nc.vector.tensor_copy(
-                        woven[:].rearrange("p c t -> p (c t)").bitcast(I32).rearrange("p (c u) -> p c u", u=2)[:, cols(h), :],
-                        src.rearrange("p u c e -> p u (c e)").bitcast(I32)[:, :, cols(h)].rearrange("p u c -> p c u"),
-                    )
-                else:
-                    nc.vector.tensor_copy(woven[:, cols(h), :], src[:, :, cols(h)].rearrange("p t c -> p c t"))
-            for h in range(2):
-                nc.vector.quantize_mx(
-                    out=codes[:, cols(h)].bitcast(FP8X4), scales=scale[:, cols(h)],
-                    in_=woven[:, cols(h), :].rearrange("p c t -> p (c t)"),
+        def turn(dst, *terms):
+            for i, term in enumerate(terms):
+                nc.tensor.matmul(
+                    dst, lhsT=term, rhs=ident[:], start=i == 0, stop=i == len(terms) - 1, is_transpose=True
                 )
 
+        def turned(index, *terms):
+            dst = bank(index)
+            for j in range(BLOCKS):
+                turn(dst[:, block(j)], *[term[:, block(j)] for term in terms])
+            return dst
+
+        def quantise(woven, codes, scale, h):
+            nc.vector.quantize_mx(
+                out=codes[:, half(h)].bitcast(FP8X4), scales=scale[:, half(h)],
+                in_=woven[:, half(h), :].rearrange("p c t -> p (c t)"),
+            )
+
+        def packed(name, dtype):
+            return (
+                sb.tile([P, S, PACK], BF16, name=f"{name}_woven", align_bytes=64),
+                sb.tile([P, S], dtype, name=f"{name}_codes", align_bytes=64),
+                sb.tile([P, S], U8, name=f"{name}_scale", align_bytes=64),
+            )
+
         xs_raw = sb.tile([P, T], U8, name="xs_raw", align_bytes=64)
-        w1s_raw = sb.tile([P, S], U8, name="w1s_raw", align_bytes=64)
+        ws_raw = sb.tile([P, S], U8, name="ws_raw", align_bytes=64)
         nc.vector.memset(xs_raw[:].bitcast(I32), 0)
-        nc.vector.memset(w1s_raw[:].bitcast(I32), 0)
-        load_scale_rows(nc.sync, xs_raw, 0, x_scales)
+        nc.vector.memset(ws_raw[:].bitcast(I32), 0)
+        load_scale_rows(xs_raw, 0, x_scales)
         w1_raw = load_words("w1_raw", w1_words)
         offs_t = load_list("offs_t", offs)
         xw_raw = load_words("xw_raw", x_words)
-        load_scale_rows(nc.sync, w1s_raw, 0, w1_scales)
+        load_scale_rows(ws_raw, 0, w1_scales)
         n4_t = load_list("n4_t", n4)
         n3_t = load_list("n3_t", n3)
         w2_raw = load_words("w2_raw", w2_words)
@@ -117,214 +131,130 @@ def tile_picked_forknormbfoldodds_none_po_kernel(
         n1_t = load_list("n1_t", n1)
         n2_t = load_list("n2_t", n2)
 
-        w1_scale = deal("w1_scale", w1s_raw, U8, nc.gpsimd)
+        w1_scale = deal("w1_scale", ws_raw, U8, nc.gpsimd)
         w1 = deal("w1", w1_raw, I32, nc.vector)
         x_scale = sb.tile([P, S], U8, name="x_scale", align_bytes=64)
         x_codes = sb.tile([P, S], U32, name="x_codes", align_bytes=64)
         nc.vector.tensor_copy(x_scale[:], xs_raw[:].indirect(offs_t[:]))
         nc.vector.tensor_copy(x_codes[:], xw_raw[:].bitcast(U32).indirect(offs_t[:]))
-        y_ps = product("lo", w1, w1_scale, 0, x_codes, x_scale)
+        y_ps = product(0, w1, w1_scale, 0, x_codes, x_scale)
 
-        y = planes("y", 2 * S)
-        ex = planes("ex", 2 * S)
-        size = planes("size", 2 * S)
-        neg_a = planes("neg_a", 2 * S)
-        ds = planes("ds")
-        e3 = planes("e3")
-        e4 = planes("e4")
-        odds = planes("odds", 2 * S)
-        pa = planes("pa", HALF)
-        gate = planes("gate", HALF)
-        neg_a2 = planes("neg_a2")
-        z_all = sb.tile([P, PACK, S], BF16, name="z_all", align_bytes=64)
-        z2_codes = sb.tile([P, S], U32, name="z2_codes", align_bytes=64)
-        z2_scale = sb.tile([P, S], U8, name="z2_scale", align_bytes=64)
-        z_codes = sb.tile([P, S], U32, name="z_codes", align_bytes=64)
-        z_scale = sb.tile([P, S], U8, name="z_scale", align_bytes=64)
-        den = sb.tile([P, PACK, S], F32, name="den", align_bytes=64)
-        diff = sb.tile([P, PACK, S], F32, name="diff", align_bytes=64)
-        out_codes = sb.tile([P, S], I32, name="out_codes", align_bytes=64)
-        out_scale = sb.tile([P, S], U8, name="out_scale", align_bytes=64)
-        out_rows = out_0.rearrange("(p t) c -> p t c", t=PACK)
-        out_words = out_1[0].rearrange("p n r -> p (n r)").bitcast(I32)
-
-        res = sb.tile([P, PACK, S], F32, name="res", align_bytes=64)
-
-        def join(t):
-            nc.vector.tensor_tensor(diff[:, t, :], neg_a[t][:].indirect(n6_t[:]), neg_a2[t][:], ALU.subtract)
-
-        def scale(t):
-            nc.vector.tensor_tensor(res[:, t, :], recip[t][:].rearrange("p j c -> p (j c)"), diff[:, t, :], ALU.mult)
-            nc.sync.dma_start(out_rows[:, t, :], res[:, t, :])
-
-        def finish():
-            woven = sb.tile([P, S, PACK], BF16, name="out_woven", align_bytes=64)
-            nc.scalar.copy(woven[:, :, 0:2], res[:, 0:2, :].rearrange("p t c -> p c t"))
-            for h in range(2):
-                nc.vector.tensor_copy(woven[:, cols(h), 2:4], res[:, 2:4, cols(h)].rearrange("p t c -> p c t"))
-            for h in range(2):
-                nc.vector.quantize_mx(
-                    out=out_codes[:, cols(h)].bitcast(FP8X4), scales=out_scale[:, cols(h)],
-                    in_=woven[:, cols(h), :].rearrange("p c t -> p (c t)"),
-                )
-                nc.sync.dma_start(out_words[:, cols(h)], out_codes[:, cols(h)])
-
-        ident = sb.tile([P, P], F32, name="ident")
+        ident = sb.tile([P, P], F32, name="ident", tag="w1_raw", align_bytes=64)
         make_identity(nc, ident[:])
-        e5 = planes("e5")
-        g7 = planes("g7")
 
-        def bank(name):
-            return ps.tile([P, PACK, P], F32, name=name, tag=name)
-
-        def turn(dst, *srcs):
-            for i, src in enumerate(srcs):
-                nc.tensor.matmul(dst, lhsT=src, rhs=ident[:], start=i == 0, stop=i == len(srcs) - 1, is_transpose=True)
-
-        def turned_sum(name, first, second):
-            dst = bank(name)
-            for j in range(PACK):
-                turn(dst[:, j, :], first[:, j * P : (j + 1) * P], second[:, j * P : (j + 1) * P])
-            return dst[:].rearrange("c j p -> c (j p)")
-
+        y = planes("y", WINDOW)
+        ex = planes("ex", WINDOW)
+        e4 = planes("e4")
         nc.scalar.activation(ex[0][:, 0:S], y_ps[0][:], ACT.Exp, scale=0.5)
-        nc.scalar.copy(y[0][:, 0:S], y_ps[0][:])
-        nc.scalar.activation(ex[1][:, 0:S], y_ps[1][:], ACT.Exp, scale=0.5)
-        nc.scalar.activation(e4[0][:], y[0][:].indirect(n4_t[:]), ACT.Exp, scale=0.5)
-        nc.scalar.copy(y[1][:, 0:S], y_ps[1][:])
-        nc.scalar.activation(ex[2][:, 0:S], y_ps[2][:], ACT.Exp, scale=0.5)
-        nc.scalar.activation(e4[1][:], y[1][:].indirect(n4_t[:]), ACT.Exp, scale=0.5)
-        nc.scalar.copy(y[2][:, 0:S], y_ps[2][:])
-        nc.scalar.activation(e4[2][:], y[2][:].indirect(n4_t[:]), ACT.Exp, scale=0.5)
-        nc.scalar.copy(y[3][:, 0:S], y_ps[3][:])
-        nc.scalar.activation(ex[3][:, 0:S], y_ps[3][:], ACT.Exp, scale=0.5)
-        nc.scalar.activation(e4[3][:], y[3][:].indirect(n4_t[:]), ACT.Exp, scale=0.5)
-        load_scale_rows(nc.sync, w1s_raw, 4, w2_scales)
-        load_scale_rows(nc.sync, w1s_raw, 8, w3_scales)
-        nc.sync.dma_start(ds[0][:], y[0][:, 0:S])
-        nc.sync.dma_start(ds[1][:], y[1][:, 0:S])
-        nc.sync.dma_start(ds[2][:], y[2][:, 0:S])
-        nc.sync.dma_start(ds[3][:], y[3][:, 0:S])
+        for t in range(PACK):
+            nc.scalar.copy(y[t][:, 0:S], y_ps[t][:])
+            if t + 1 < PACK:
+                nc.scalar.activation(ex[t + 1][:, 0:S], y_ps[t + 1][:], ACT.Exp, scale=0.5)
+            if t < SCALAR_N4:
+                nc.scalar.activation(e4[t][:], y[t][:].indirect(n4_t[:]), ACT.Exp, scale=0.5)
+
+        load_scale_rows(ws_raw, W2_ROW, w2_scales)
+        load_scale_rows(ws_raw, W3_ROW, w3_scales)
+        ds = planes("ds")
+        for t in range(PACK):
+            nc.sync.dma_start(ds[t][:], y[t][:, 0:S])
         gn_t = load_gain("gn_t", gn)
         gm_t = load_gain("gm_t", gm)
         n6_t = load_list("n6_t", n6)
         n7_t = load_list("n7_t", n7)
-        nc.vector.tensor_copy(e3[0][:], ex[0][:].indirect(n3_t[:]))
-        nc.vector.tensor_copy(e5[0][:], ex[0][:].indirect(n5_t[:]))
-        nc.vector.tensor_copy(pa[0][:], y[0][:].indirect(n1_t[:]))
-        nc.vector.tensor_copy(e3[1][:], ex[1][:].indirect(n3_t[:]))
-        nc.vector.tensor_copy(e5[1][:], ex[1][:].indirect(n5_t[:]))
-        nc.vector.tensor_copy(pa[1][:], y[1][:].indirect(n1_t[:]))
-        nc.vector.tensor_copy(e3[2][:], ex[2][:].indirect(n3_t[:]))
-        nc.vector.tensor_copy(e5[2][:], ex[2][:].indirect(n5_t[:]))
-        nc.vector.tensor_copy(pa[2][:], y[2][:].indirect(n1_t[:]))
-        nc.vector.tensor_copy(e3[3][:], ex[3][:].indirect(n3_t[:]))
-        nc.vector.tensor_copy(e5[3][:], ex[3][:].indirect(n5_t[:]))
-        nc.vector.tensor_copy(pa[3][:], y[3][:].indirect(n1_t[:]))
-        nc.scalar.activation(gate[0][:], y[0][:].indirect(n2_t[:]), ACT.Sigmoid)
-        nc.scalar.activation(gate[1][:], y[1][:].indirect(n2_t[:]), ACT.Sigmoid)
-        nc.scalar.activation(gate[2][:], y[2][:].indirect(n2_t[:]), ACT.Sigmoid)
-        nc.scalar.activation(gate[3][:], y[3][:].indirect(n2_t[:]), ACT.Sigmoid)
+
+        e3 = planes("e3")
+        e5 = planes("e5")
+        pa = planes("pa", HALF)
+        gate = planes("gate", HALF)
+        for t in range(PACK):
+            nc.vector.tensor_copy(e3[t][:], ex[t][:].indirect(n3_t[:]))
+            nc.vector.tensor_copy(e5[t][:], ex[t][:].indirect(n5_t[:]))
+            if t >= SCALAR_N4:
+                nc.vector.tensor_copy(e4[t][:], ex[t][:].indirect(n4_t[:]))
+            nc.vector.tensor_copy(pa[t][:], y[t][:].indirect(n1_t[:]))
+        for t in range(PACK):
+            nc.scalar.activation(gate[t][:], y[t][:].indirect(n2_t[:]), ACT.Sigmoid)
         w2 = deal("w2", w2_raw, I32, nc.vector)
         w3 = deal("w3", w3_raw, I32, nc.vector)
-        w23_scale = deal("w23_scale", w1s_raw, U8, nc.gpsimd)
-        below = turned_sum("hi0", e4[0][:], e5[0][:])
-        above = turned_sum("hi1", ex[0][:, 0:S], e3[0][:])
-        nc.scalar.activation(odds[0][:, S : 2 * S], below, ACT.Ln)
-        nc.gpsimd.tensor_scalar(odds[0][:, S : 2 * S], odds[0][:, S : 2 * S], -1.0, 0.0, ALU.mult, ALU.add)
-        nc.scalar.activation(odds[0][:, 0:S], above, ACT.Ln)
-        below = turned_sum("hi2", e4[1][:], e5[1][:])
-        above = turned_sum("hi3", ex[1][:, 0:S], e3[1][:])
-        nc.scalar.activation(odds[1][:, S : 2 * S], below, ACT.Ln)
-        nc.gpsimd.tensor_scalar(odds[1][:, S : 2 * S], odds[1][:, S : 2 * S], -1.0, 0.0, ALU.mult, ALU.add)
-        nc.scalar.activation(odds[1][:, 0:S], above, ACT.Ln)
-        below = turned_sum("lo0", e4[2][:], e5[2][:])
-        above = turned_sum("lo1", ex[2][:, 0:S], e3[2][:])
-        nc.scalar.activation(odds[2][:, S : 2 * S], below, ACT.Ln)
-        nc.gpsimd.tensor_scalar(odds[2][:, S : 2 * S], odds[2][:, S : 2 * S], -1.0, 0.0, ALU.mult, ALU.add)
-        nc.scalar.activation(odds[2][:, 0:S], above, ACT.Ln)
-        below = turned_sum("lo2", e4[3][:], e5[3][:])
-        above = turned_sum("lo3", ex[3][:, 0:S], e3[3][:])
-        nc.scalar.activation(odds[3][:, S : 2 * S], below, ACT.Ln)
-        nc.gpsimd.tensor_scalar(odds[3][:, S : 2 * S], odds[3][:, S : 2 * S], -1.0, 0.0, ALU.mult, ALU.add)
-        nc.scalar.activation(odds[3][:, 0:S], above, ACT.Ln)
-        nc.vector.tensor_tensor(ds[0][:].indirect(n2_t[:]), pa[0][:], gate[0][:], ALU.mult)
-        nc.vector.tensor_tensor(ds[1][:].indirect(n2_t[:]), pa[1][:], gate[1][:], ALU.mult)
-        nc.vector.tensor_tensor(ds[2][:].indirect(n2_t[:]), pa[2][:], gate[2][:], ALU.mult)
-        nc.vector.tensor_tensor(ds[3][:].indirect(n2_t[:]), pa[3][:], gate[3][:], ALU.mult)
-        nc.scalar.activation(z_all[:, 0, :], ds[0][:], ACT.Copy, scale=gn_t[:, 0 : 1])
-        nc.scalar.activation(z_all[:, 1, :], ds[1][:], ACT.Copy, scale=gn_t[:, 1 : 2])
-        nc.scalar.activation(z_all[:, 2, :], ds[2][:], ACT.Copy, scale=gn_t[:, 2 : 3])
-        nc.scalar.activation(z_all[:, 3, :], ds[3][:], ACT.Copy, scale=gn_t[:, 3 : 4])
-        back = [bank(f"hi{j}") for j in range(PACK)]
+        w23_scale = deal("w23_scale", ws_raw, U8, nc.gpsimd)
+
+        log_above = planes("log_above")
+        log_below = planes("log_below")
         for t in range(PACK):
-            for j in range(PACK):
-                turn(back[j][:, t, :], odds[t][:, j * P : (j + 1) * P], odds[t][:, S + j * P : S + (j + 1) * P])
-        z2_woven = sb.tile([P, S, PACK], BF16, name="z2_woven", align_bytes=64)
-        for j in range(PACK):
+            below = turned((PACK + 2 * t) % (2 * PACK), e4[t], e5[t])
+            above = turned((PACK + 2 * t + 1) % (2 * PACK), ex[t], e3[t])
+            nc.scalar.activation(log_below[t][:], below[:], ACT.Ln)
+            nc.scalar.activation(log_above[t][:], above[:], ACT.Ln)
+            nc.scalar.activation(log_below[t][:], log_below[t][:], ACT.Copy, scale=-1.0)
+
+        for t in range(PACK):
+            nc.vector.tensor_tensor(ds[t][:].indirect(n2_t[:]), pa[t][:], gate[t][:], ALU.mult)
+        z = sb.tile([P, PACK, S], BF16, name="z", align_bytes=64)
+        for t in range(PACK):
+            nc.scalar.activation(z[:, t, :], ds[t][:], ACT.Copy, scale=gn_t[:, t : t + 1])
+
+        log_odds = [bank(PACK + j) for j in range(BLOCKS)]
+        for t in range(PACK):
+            for j in range(BLOCKS):
+                turn(log_odds[j][:, block(t)], log_above[t][:, block(j)], log_below[t][:, block(j)])
+        z2_woven, z2_codes, z2_scale = packed("z2", U32)
+        for j in range(BLOCKS):
             nc.vector.tensor_tensor(
-                z2_woven[:, j * P : (j + 1) * P, :], back[j][:].rearrange("p t c -> p c t"),
+                z2_woven[:, block(j), :], log_odds[j][:].rearrange("p (t c) -> p c t", t=PACK),
                 gm_t[:].unsqueeze(1).to_broadcast([P, P, PACK]), ALU.mult,
             )
         for h in range(2):
-            nc.vector.quantize_mx(
-                out=z2_codes[:, cols(h)].bitcast(FP8X4), scales=z2_scale[:, cols(h)],
-                in_=z2_woven[:, cols(h), :].rearrange("p c t -> p (c t)"),
-            )
-        b_ps = product("lo", w3, w23_scale, 8, z2_codes, z2_scale)
-        quantise("z_woven", z_all[:], z_codes[:], z_scale[:])
-        a_ps = product("hi", w2, w23_scale, 4, z_codes, z_scale)
-        nc.scalar.activation(size[0][:, 0:S], b_ps[0][:], ACT.Abs)
-        nc.scalar.activation(size[1][:, 0:S], b_ps[1][:], ACT.Abs)
-        nc.scalar.activation(neg_a[0][:, 0:S], a_ps[0][:], ACT.Copy, scale=-1.0)
-        nc.sync.dma_start(neg_a2[0][:], neg_a[0][:, 0:S])
-        nc.scalar.activation(size[2][:, 0:S], b_ps[2][:], ACT.Abs)
-        nc.scalar.activation(neg_a[1][:, 0:S], a_ps[1][:], ACT.Copy, scale=-1.0)
-        nc.sync.dma_start(neg_a2[1][:], neg_a[1][:, 0:S])
-        nc.scalar.activation(size[3][:, 0:S], b_ps[3][:], ACT.Abs)
-        nc.scalar.activation(neg_a[2][:, 0:S], a_ps[2][:], ACT.Copy, scale=-1.0)
-        nc.sync.dma_start(neg_a2[2][:], neg_a[2][:, 0:S])
-        nc.scalar.activation(neg_a[3][:, 0:S], a_ps[3][:], ACT.Copy, scale=-1.0)
-        nc.sync.dma_start(neg_a2[3][:], neg_a[3][:, 0:S])
-        nc.vector.tensor_copy(g7[0][:], size[0][:].indirect(n7_t[:]))
-        nc.vector.tensor_copy(g7[1][:], size[1][:].indirect(n7_t[:]))
-        nc.vector.tensor_copy(g7[2][:], size[2][:].indirect(n7_t[:]))
-        nc.vector.tensor_copy(g7[3][:], size[3][:].indirect(n7_t[:]))
-        recip = []
-        total = turned_sum("lo0", size[0][:, 0:S], g7[0][:])
-        nc.scalar.activation(den[:, 0, :], total, ACT.Abs_reciprocal_sqrt, bias=0.5)
-        total = turned_sum("lo1", size[1][:, 0:S], g7[1][:])
-        nc.scalar.activation(den[:, 1, :], total, ACT.Abs_reciprocal_sqrt, bias=0.5)
-        total = turned_sum("lo2", size[2][:, 0:S], g7[2][:])
-        nc.scalar.activation(den[:, 2, :], total, ACT.Abs_reciprocal_sqrt, bias=0.5)
-        total = turned_sum("lo3", size[3][:, 0:S], g7[3][:])
-        nc.scalar.activation(den[:, 3, :], total, ACT.Abs_reciprocal_sqrt, bias=0.5)
-        nc.scalar.activation(den[:, 0, :], den[:, 0, :], ACT.Square)
-        recip.append(bank("hi0"))
-        for j in range(PACK):
-            turn(recip[0][:, j, :], den[:, 0, j * P : (j + 1) * P])
-        nc.scalar.activation(den[:, 1, :], den[:, 1, :], ACT.Square)
-        recip.append(bank("hi1"))
-        for j in range(PACK):
-            turn(recip[1][:, j, :], den[:, 1, j * P : (j + 1) * P])
-        nc.scalar.activation(den[:, 2, :], den[:, 2, :], ACT.Square)
-        recip.append(bank("hi2"))
-        for j in range(PACK):
-            turn(recip[2][:, j, :], den[:, 2, j * P : (j + 1) * P])
-        nc.scalar.activation(den[:, 3, :], den[:, 3, :], ACT.Square)
-        recip.append(bank("hi3"))
-        for j in range(PACK):
-            turn(recip[3][:, j, :], den[:, 3, j * P : (j + 1) * P])
-        join(0)
-        join(1)
-        join(2)
-        scale(0)
-        join(3)
-        scale(1)
-        scale(2)
-        scale(3)
-        finish()
-        for q in range(4):
+            quantise(z2_woven, z2_codes, z2_scale, h)
+        b_ps = product(0, w3, w23_scale, W3_ROW, z2_codes, z2_scale)
+
+        z_woven, z_codes, z_scale = packed("z", U32)
+        for h in range(2):
+            nc.vector.tensor_copy(z_woven[:, half(h), :], z[:, :, half(h)].rearrange("p t c -> p c t"))
+        for h in range(2):
+            quantise(z_woven, z_codes, z_scale, h)
+        a_ps = product(PACK, w2, w23_scale, W2_ROW, z_codes, z_scale)
+
+        size = planes("size", WINDOW)
+        neg_a = planes("neg_a", WINDOW)
+        neg_a_copy = planes("neg_a_copy")
+        for t in range(PACK):
+            nc.scalar.activation(size[t][:, 0:S], b_ps[t][:], ACT.Abs)
+        for t in range(PACK):
+            nc.scalar.activation(neg_a[t][:, 0:S], a_ps[t][:], ACT.Copy, scale=-1.0)
+            nc.sync.dma_start(neg_a_copy[t][:], neg_a[t][:, 0:S])
+
+        size7 = planes("size7")
+        root = planes("root")
+        for t in range(PACK):
+            nc.vector.tensor_copy(size7[t][:], size[t][:].indirect(n7_t[:]))
+        reciprocal = []
+        for t in range(PACK + 1):
+            if t < PACK:
+                total = turned(t, size[t], size7[t])
+                nc.scalar.activation(root[t][:], total[:], ACT.Abs_reciprocal_sqrt, bias=0.5)
+            if t > 0:
+                nc.scalar.activation(root[t - 1][:], root[t - 1][:], ACT.Square)
+                reciprocal.append(turned(PACK + t - 1, root[t - 1]))
+
+        diff = planes("diff")
+        for t in range(PACK):
+            nc.vector.tensor_tensor(diff[t][:], neg_a[t][:].indirect(n6_t[:]), neg_a_copy[t][:], ALU.subtract)
+        res = sb.tile([P, PACK, S], F32, name="res", align_bytes=64)
+        out_rows = out_0.rearrange("(p t) c -> p t c", t=PACK)
+        for t in range(PACK):
+            nc.vector.tensor_tensor(res[:, t, :], reciprocal[t][:], diff[t][:], ALU.mult)
+            nc.sync.dma_start(out_rows[:, t, :], res[:, t, :])
+
+        out_woven, out_codes, out_scale = packed("out", I32)
+        out_words = out_1[0].rearrange("p n r -> p (n r)").bitcast(I32)
+        nc.scalar.copy(out_woven[:, :, 0:2], res[:, 0:2, :].rearrange("p t c -> p c t"))
+        for h in range(2):
+            nc.vector.tensor_copy(out_woven[:, half(h), 2:4], res[:, 2:4, half(h)].rearrange("p t c -> p c t"))
+        for h in range(2):
+            quantise(out_woven, out_codes, out_scale, h)
+            nc.sync.dma_start(out_words[:, half(h)], out_codes[:, half(h)])
+        for q in range(QUADRANTS):
             queue = nc.sync if q % 2 == 0 else nc.scalar
             queue.dma_start(
                 out_2[0, 4 * q : 4 * q + 4, :].bitcast(I32), out_scale[32 * q : 32 * q + 4, :].bitcast(I32)

from contextlib import ExitStack

import concourse.mybir as mybir
from concourse.masks import make_identity

F32 = mybir.dt.float32
BF16 = mybir.dt.bfloat16
I32 = mybir.dt.int32
U32 = mybir.dt.uint32
U16 = mybir.dt.uint16
U8 = mybir.dt.uint8
FP8X4 = mybir.dt.float8_e4m3fn_x4
ACT = mybir.ActivationFunctionType
ALU = mybir.AluOpType

P = 128
PACK = 4
QUADRANTS = 4
T = 2048
S = 512
BLOCKS = S // P
HALF = S // 2
WINDOW = 2 * S
SCALAR_N4 = 3
W2_ROW, W3_ROW = 4, 8

FLOPS = 3 * 2 * S * S * S


def tile_picked_forknormbfoldodds_none_po_kernel(
    tc, x_words, x_scales, w1_words, w1_scales, gn, w2_words, w2_scales, gm, w3_words, w3_scales,
    offs, n1, n2, n3, n4, n5, n6, n7, out_0, out_1, out_2,
):
    nc = tc.nc
    with ExitStack() as ctx:
        sb = ctx.enter_context(tc.tile_pool(name="sb", bufs=1))
        ps = ctx.enter_context(tc.psum_pool(name="ps", bufs=1))

        def planes(name, width=S):
            return [sb.tile([P, width], F32, name=f"{name}{t}", align_bytes=64) for t in range(PACK)]

        def bank(index):
            return ps.tile([P, S], F32, name=f"bank{index}", tag=f"bank{index}")

        def block(j):
            return slice(j * P, (j + 1) * P)

        def half(h):
            return slice(h * HALF, (h + 1) * HALF)

        def load_list(name, src):
            tile = sb.tile(list(src.shape), U16, name=name)
            nc.sync.dma_start(tile[:], src)
            return tile

        def load_words(name, src):
            tile = sb.tile([P, src.shape[2]], I32, name=name, align_bytes=64)
            nc.sync.dma_start(tile[:], src[0].rearrange("p n r -> p (n r)").bitcast(I32))
            return tile

        def load_scale_rows(tile, first, src):
            for q in range(QUADRANTS):
                nc.sync.dma_start(
                    tile[32 * q + first : 32 * q + first + 4, :].bitcast(I32),
                    src[0, 4 * q : 4 * q + 4, :].bitcast(I32),
                )

        def load_gain(name, src):
            tile = sb.tile([P, PACK], F32, name=name)
            nc.sync.dma_start(tile[:], src.rearrange("(p t) o -> p (t o)", t=PACK))
            return tile

        def deal(name, src, dtype, engine):
            tile = sb.tile([P, S], dtype, name=name, align_bytes=64)
            engine.tensor_copy(
                tile[:].rearrange("p (t m) -> p t m", t=PACK),
                src[:].rearrange("p (m t) -> p t m", t=PACK),
            )
            return tile

        def product(first_bank, w, w_scale, first_row, codes, scale):
            result = []
            for t in range(PACK):
                plane = bank(first_bank + t)
                nc.tensor.matmul_mx(
                    out=plane[:], lhsT=w[:, block(t)].bitcast(FP8X4), lhsT_scale=w_scale[first_row:P, block(t)],
                    rhs=codes[:].bitcast(FP8X4), rhs_scale=scale[:], start=True, stop=True,
                )
                result.append(plane)
            return result

        def turn(dst, *terms):
            for i, term in enumerate(terms):
                nc.tensor.matmul(
                    dst, lhsT=term, rhs=ident[:], start=i == 0, stop=i == len(terms) - 1, is_transpose=True
                )

        def turned(index, *terms):
            dst = bank(index)
            for j in range(BLOCKS):
                turn(dst[:, block(j)], *[term[:, block(j)] for term in terms])
            return dst

        def quantise(woven, codes, scale, h):
            nc.vector.quantize_mx(
                out=codes[:, half(h)].bitcast(FP8X4), scales=scale[:, half(h)],
                in_=woven[:, half(h), :].rearrange("p c t -> p (c t)"),
            )

        def packed(name, dtype):
            return (
                sb.tile([P, S, PACK], BF16, name=f"{name}_woven", align_bytes=64),
                sb.tile([P, S], dtype, name=f"{name}_codes", align_bytes=64),
                sb.tile([P, S], U8, name=f"{name}_scale", align_bytes=64),
            )

        xs_raw = sb.tile([P, T], U8, name="xs_raw", align_bytes=64)
        ws_raw = sb.tile([P, S], U8, name="ws_raw", align_bytes=64)
        nc.vector.memset(xs_raw[:].bitcast(I32), 0)
        nc.vector.memset(ws_raw[:].bitcast(I32), 0)
        load_scale_rows(xs_raw, 0, x_scales)
        w1_raw = load_words("w1_raw", w1_words)
        offs_t = load_list("offs_t", offs)
        xw_raw = load_words("xw_raw", x_words)
        load_scale_rows(ws_raw, 0, w1_scales)
        n4_t = load_list("n4_t", n4)
        n3_t = load_list("n3_t", n3)
        w2_raw = load_words("w2_raw", w2_words)
        n5_t = load_list("n5_t", n5)
        w3_raw = load_words("w3_raw", w3_words)
        n1_t = load_list("n1_t", n1)
        n2_t = load_list("n2_t", n2)

        w1_scale = deal("w1_scale", ws_raw, U8, nc.gpsimd)
        w1 = deal("w1", w1_raw, I32, nc.vector)
        x_scale = sb.tile([P, S], U8, name="x_scale", align_bytes=64)
        x_codes = sb.tile([P, S], U32, name="x_codes", align_bytes=64)
        nc.vector.tensor_copy(x_scale[:], xs_raw[:].indirect(offs_t[:]))
        nc.vector.tensor_copy(x_codes[:], xw_raw[:].bitcast(U32).indirect(offs_t[:]))
        y_ps = product(0, w1, w1_scale, 0, x_codes, x_scale)

        ident = sb.tile([P, P], F32, name="ident", tag="w1_raw", align_bytes=64)
        make_identity(nc, ident[:])

        y = planes("y", WINDOW)
        ex = planes("ex", WINDOW)
        e4 = planes("e4")
        nc.scalar.activation(ex[0][:, 0:S], y_ps[0][:], ACT.Exp, scale=0.5)
        for t in range(PACK):
            nc.scalar.copy(y[t][:, 0:S], y_ps[t][:])
            if t + 1 < PACK:
                nc.scalar.activation(ex[t + 1][:, 0:S], y_ps[t + 1][:], ACT.Exp, scale=0.5)
            if t < SCALAR_N4:
                nc.scalar.activation(e4[t][:], y[t][:].indirect(n4_t[:]), ACT.Exp, scale=0.5)

        load_scale_rows(ws_raw, W2_ROW, w2_scales)
        load_scale_rows(ws_raw, W3_ROW, w3_scales)
        ds = planes("ds")
        for t in range(PACK):
            nc.sync.dma_start(ds[t][:], y[t][:, 0:S])
        gn_t = load_gain("gn_t", gn)
        gm_t = load_gain("gm_t", gm)
        n6_t = load_list("n6_t", n6)
        n7_t = load_list("n7_t", n7)

        e3 = planes("e3")
        e5 = planes("e5")
        pa = planes("pa", HALF)
        gate = planes("gate", HALF)
        for t in range(PACK):
            nc.vector.tensor_copy(e3[t][:], ex[t][:].indirect(n3_t[:]))
            nc.vector.tensor_copy(e5[t][:], ex[t][:].indirect(n5_t[:]))
            if t >= SCALAR_N4:
                nc.vector.tensor_copy(e4[t][:], ex[t][:].indirect(n4_t[:]))
            nc.vector.tensor_copy(pa[t][:], y[t][:].indirect(n1_t[:]))
        for t in range(PACK):
            nc.scalar.activation(gate[t][:], y[t][:].indirect(n2_t[:]), ACT.Sigmoid)
        w2 = deal("w2", w2_raw, I32, nc.vector)
        w3 = deal("w3", w3_raw, I32, nc.vector)
        w23_scale = deal("w23_scale", ws_raw, U8, nc.gpsimd)

        log_above = planes("log_above")
        log_below = planes("log_below")
        for t in range(PACK):
            below = turned((PACK + 2 * t) % (2 * PACK), e4[t], e5[t])
            above = turned((PACK + 2 * t + 1) % (2 * PACK), ex[t], e3[t])
            nc.scalar.activation(log_below[t][:], below[:], ACT.Ln)
            nc.scalar.activation(log_above[t][:], above[:], ACT.Ln)
            nc.scalar.activation(log_below[t][:], log_below[t][:], ACT.Copy, scale=-1.0)

        for t in range(PACK):
            nc.vector.tensor_tensor(ds[t][:].indirect(n2_t[:]), pa[t][:], gate[t][:], ALU.mult)
        z = sb.tile([P, PACK, S], BF16, name="z", align_bytes=64)
        for t in range(PACK):
            nc.scalar.activation(z[:, t, :], ds[t][:], ACT.Copy, scale=gn_t[:, t : t + 1])

        log_odds = [bank(PACK + j) for j in range(BLOCKS)]
        for t in range(PACK):
            for j in range(BLOCKS):
                turn(log_odds[j][:, block(t)], log_above[t][:, block(j)], log_below[t][:, block(j)])
        z2_woven, z2_codes, z2_scale = packed("z2", U32)
        for j in range(BLOCKS):
            nc.vector.tensor_tensor(
                z2_woven[:, block(j), :], log_odds[j][:].rearrange("p (t c) -> p c t", t=PACK),
                gm_t[:].unsqueeze(1).to_broadcast([P, P, PACK]), ALU.mult,
            )
        for h in range(2):
            quantise(z2_woven, z2_codes, z2_scale, h)
        b_ps = product(0, w3, w23_scale, W3_ROW, z2_codes, z2_scale)

        z_woven, z_codes, z_scale = packed("z", U32)
        for h in range(2):
            nc.vector.tensor_copy(z_woven[:, half(h), :], z[:, :, half(h)].rearrange("p t c -> p c t"))
        for h in range(2):
            quantise(z_woven, z_codes, z_scale, h)
        a_ps = product(PACK, w2, w23_scale, W2_ROW, z_codes, z_scale)

        size = planes("size", WINDOW)
        neg_a = planes("neg_a", WINDOW)
        neg_a_copy = planes("neg_a_copy")
        for t in range(PACK):
            nc.scalar.activation(size[t][:, 0:S], b_ps[t][:], ACT.Abs)
        for t in range(PACK):
            nc.scalar.activation(neg_a[t][:, 0:S], a_ps[t][:], ACT.Copy, scale=-1.0)
            nc.sync.dma_start(neg_a_copy[t][:], neg_a[t][:, 0:S])

        size7 = planes("size7")
        root = planes("root")
        for t in range(PACK):
            nc.vector.tensor_copy(size7[t][:], size[t][:].indirect(n7_t[:]))
        reciprocal = []
        for t in range(PACK + 1):
            if t < PACK:
                total = turned(t, size[t], size7[t])
                nc.scalar.activation(root[t][:], total[:], ACT.Abs_reciprocal_sqrt, bias=0.5)
            if t > 0:
                nc.scalar.activation(root[t - 1][:], root[t - 1][:], ACT.Square)
                reciprocal.append(turned(PACK + t - 1, root[t - 1]))

        diff = planes("diff")
        for t in range(PACK):
            nc.vector.tensor_tensor(diff[t][:], neg_a[t][:].indirect(n6_t[:]), neg_a_copy[t][:], ALU.subtract)
        res = sb.tile([P, PACK, S], F32, name="res", align_bytes=64)
        out_rows = out_0.rearrange("(p t) c -> p t c", t=PACK)
        for t in range(PACK):
            nc.vector.tensor_tensor(res[:, t, :], reciprocal[t][:], diff[t][:], ALU.mult)
            nc.sync.dma_start(out_rows[:, t, :], res[:, t, :])

        out_woven, out_codes, out_scale = packed("out", I32)
        out_words = out_1[0].rearrange("p n r -> p (n r)").bitcast(I32)
        nc.scalar.copy(out_woven[:, :, 0:2], res[:, 0:2, :].rearrange("p t c -> p c t"))
        for h in range(2):
            nc.vector.tensor_copy(out_woven[:, half(h), 2:4], res[:, 2:4, half(h)].rearrange("p t c -> p c t"))
        for h in range(2):
            quantise(out_woven, out_codes, out_scale, h)
            nc.sync.dma_start(out_words[:, half(h)], out_codes[:, half(h)])
        for q in range(QUADRANTS):
            queue = nc.sync if q % 2 == 0 else nc.scalar
            queue.dma_start(
                out_2[0, 4 * q : 4 * q + 4, :].bitcast(I32), out_scale[32 * q : 32 * q + 4, :].bitcast(I32)
            )
